import numpy as np
import ml_dtypes


def mxq(x, axis, fmt="e4m3"):
    dtype, down = {"e4m3": (ml_dtypes.float8_e4m3fn, 7), "e5m2": (ml_dtypes.float8_e5m2, 14)}[fmt]
    v = np.moveaxis(np.asarray(x, np.float32).astype(ml_dtypes.bfloat16).astype(np.float64), axis, -1)
    blocks = v.reshape(v.shape[:-1] + (-1, 32))
    amax = np.abs(blocks).max(-1, keepdims=True)
    byte = np.maximum(np.where(amax > 0, np.frexp(amax)[1] - 1 + 127, 0) - down, 1)
    scale = np.exp2(byte - 127.0)
    codes = (blocks / scale).astype(np.float32).astype(dtype).astype(np.float64)
    return np.moveaxis((codes * scale).reshape(v.shape), -1, axis)


WIDE = False


def mx_kscale(k):
    if not WIDE:
        return np.ones(k)
    levels = np.array([10, -10, 5, -5, 0])
    if k % 512:
        return np.exp2(np.random.permutation(np.resize(levels, k // 32))).repeat(32)
    a = np.empty((k // 512, 16))
    for p in range(k // 512):
        a[p, :8] = np.random.permutation(np.resize(levels, 8))
        for g in range(8):
            far = levels[np.abs(levels - a[p, g]) >= 10]
            a[p, g + 8] = far[np.random.randint(len(far))]
    return np.exp2(a.ravel()).repeat(32)


def f64(x):
    return np.asarray(x).astype(np.float64)


def striped(idx):
    return np.tile(idx.reshape(-1, 16).T, (8, 1)).astype(np.uint16)


def unstriped(offs):
    return offs[:16].T.reshape(-1).astype(np.int64)


def pack_weight(w):
    k, n = w.shape
    w = f64(np.asarray(w, np.float32).astype(ml_dtypes.bfloat16)).reshape(k // 32, 32, n)
    amax = np.abs(w).max(1)
    byte = np.clip(np.where(amax > 0, np.frexp(amax)[1] - 1 + 127 - 7, 1), 1, 254)
    scaled = (w * np.exp2(127.0 - byte)[:, None, :]).reshape(k, n).astype(np.float32)
    words = np.ascontiguousarray(scaled.reshape(k // 512, 128, 4, n).transpose(0, 1, 3, 2)).astype(ml_dtypes.float8_e4m3fn).view(np.uint8)
    return words, np.ascontiguousarray(byte.astype(np.uint8).reshape(k // 512, 16, n))


def unpack_weight(words, scales):
    g, p, n, _ = words.shape
    vals = np.ascontiguousarray(words).view(ml_dtypes.float8_e4m3fn).astype(np.float64) * np.repeat(np.exp2(scales.astype(np.float64) - 127.0), 8, axis=1)[..., None]
    return vals.transpose(0, 1, 3, 2).reshape(g * 512, n)


def relu(v):
    return np.maximum(v, 0.0)


K, T, S, H, N = 512, 4096, 1024, 512, 256


def setup_inputs():
    n = np.random.standard_normal
    s = mx_kscale(K)[:, None]
    u = mx_kscale(H)
    packed_xT = pack_weight(n((K, T)) * s)
    return {
        "x_words": packed_xT[0],
        "x_scales": packed_xT[1],
        "w1": (n((K, N)) / np.sqrt(2 * K) / s).astype(np.float32),
        "w2": (n((K, H)) / np.sqrt(K) / s * u).astype(np.float32),
        "w3": (n((H, N)) / np.sqrt(2 * H) / u[:, None]).astype(np.float32),
        "offs": striped(np.random.permutation(T)[:S]),
    }


def reference(x_words, x_scales, w1, w2, w3, offs):
    xq = unpack_weight(x_words, x_scales)[:, unstriped(offs)]
    h = relu(mxq(f64(w2), 0, "e4m3").T @ xq)
    return mxq(f64(w1), 0, "e4m3").T @ xq + mxq(f64(w3), 0, "e4m3").T @ mxq(h, 0, "e4m3")

@@ -1,0 +1,152 @@
+from contextlib import ExitStack
+
+import concourse.mybir as mybir
+
+K, T, S, H, N = 512, 4096, 1024, 512, 256
+FLOPS = 2 * S * (K * H + K * N + H * N)
+
+F32 = mybir.dt.float32
+BF16 = mybir.dt.bfloat16
+I32 = mybir.dt.int32
+U32 = mybir.dt.uint32
+U16 = mybir.dt.uint16
+U8 = mybir.dt.uint8
+FP8X4 = mybir.dt.float8_e4m3fn_x4
+RELU = mybir.ActivationFunctionType.Relu
+
+P = 128
+PACK = 4
+GATHER = 512
+BANK_TOKENS = 128
+CHUNK = 256
+VECTOR_H_BANKS = (5, 7)
+VECTOR_OUT_CHUNKS = (2,)
+
+
+def tile_picked_lora_relu_p_kernel(tc, x_words, x_scales, w1, w2, w3, offs, out):
+    nc = tc.nc
+    with ExitStack() as ctx:
+        keep = ctx.enter_context(tc.tile_pool(name="keep", bufs=1))
+        psum_h = ctx.enter_context(tc.psum_pool(name="psum_h", bufs=4))
+        psum_o = ctx.enter_context(tc.psum_pool(name="psum_o", bufs=4))
+
+        offsets = keep.tile([P, S // 16], U16, name="offsets")
+        nc.sync.dma_start(offsets[:], offs)
+
+        scale_table = keep.tile([P, T], U8, name="scale_table", align_bytes=64)
+        nc.sync.dma_start(scale_table[P - 16 : P, :].bitcast(I32), x_scales[0].bitcast(I32))
+        nc.vector.memset(scale_table[0 : P - 16, :].bitcast(I32), 0)
+
+        word_table = keep.tile([P, T], I32, name="word_table", align_bytes=64)
+        nc.sync.dma_start(word_table[:], x_words[0].rearrange("p n t -> p (n t)").bitcast(I32))
+
+        w2_rows = w2.rearrange("(p j) c -> p j c", j=PACK)
+        w2_raw = []
+        for half in range(2):
+            raw = keep.tile([P, PACK, H // 2], F32, name=f"w2_raw{half}")
+            nc.sync.dma_start(raw[:], w2_rows[:, :, half * (H // 2) : (half + 1) * (H // 2)])
+            w2_raw.append(raw)
+        w3_raw = keep.tile([P, PACK, N], F32, name="w3_raw")
+        nc.sync.dma_start(w3_raw[:], w3.rearrange("(p j) c -> p j c", j=PACK))
+        w1_raw = keep.tile([P, PACK, N], F32, name="w1_raw")
+        nc.sync.dma_start(w1_raw[:], w1.rearrange("(p j) c -> p j c", j=PACK))
+
+        picked_bytes = keep.tile([P, S], U8, name="picked_bytes", align_bytes=64)
+        nc.vector.tensor_copy(picked_bytes[:], scale_table[:].indirect(offsets[:]))
+        x_plane = keep.tile([P, S], U8, name="x_plane", align_bytes=64)
+        nc.vector.memset(x_plane[:].bitcast(I32), 0)
+        for r in range(4):
+            nc.scalar.dma_start(x_plane[r:P:32, :].bitcast(I32), picked_bytes[P - 16 + r : P : 4, :].bitcast(I32))
+
+        x_codes = []
+        for g in range(S // GATHER):
+            codes = keep.tile([P, GATHER], U32, name=f"x_codes{g}", align_bytes=64)
+            cols = slice(g * GATHER // 16, (g + 1) * GATHER // 16)
+            nc.vector.tensor_copy(codes[:], word_table[:].bitcast(U32).indirect(offsets[:, cols]))
+            x_codes.append(codes)
+
+        def x_operand(first, count):
+            g, lo = divmod(first, GATHER)
+            return x_codes[g][:, lo : lo + count].bitcast(FP8X4), x_plane[:, first : first + count]
+
+        w2_grouped = keep.tile([P, PACK, P, PACK], BF16, name="w2_grouped", align_bytes=64)
+
+        def cast_w2(engine_copy, half, lo, hi):
+            dst = w2_grouped[:, :, half * 64 + lo : half * 64 + hi, :].rearrange("p t m j -> p m t j")
+            src = w2_raw[half][:, :, lo * PACK : hi * PACK].rearrange("p j (m t) -> p m t j", t=PACK)
+            engine_copy(dst, src)
+
+        cast_w2(nc.scalar.copy, 0, 0, 64)
+        cast_w2(nc.vector.tensor_copy, 1, 0, 40)
+        cast_w2(nc.scalar.copy, 1, 40, 64)
+        w2_codes = keep.tile([P, H], U32, name="w2_codes", align_bytes=64)
+        w2_plane = keep.tile([P, H], U8, name="w2_plane", align_bytes=64)
+        nc.vector.quantize_mx(w2_codes[:].bitcast(FP8X4), w2_plane[:], w2_grouped[:].rearrange("p t m j -> p (t m j)"))
+
+        def cast_plain(raw, name):
+            grouped = keep.tile([P, N, PACK], BF16, name=name, align_bytes=64)
+            nc.vector.tensor_copy(
+                grouped[:].rearrange("p (c i) j -> p c j i", i=4), raw[:].rearrange("p j (c i) -> p c j i", i=4)
+            )
+            return grouped
+
+        def quantize(grouped, width, name):
+            codes = keep.tile([P, width], U32, name=name + "_codes", align_bytes=64)
+            plane = keep.tile([P, width], U8, name=name + "_plane", align_bytes=64)
+            nc.vector.quantize_mx(codes[:].bitcast(FP8X4), plane[:], grouped[:].rearrange("p c j -> p (c j)"))
+            return codes, plane
+
+        h_grouped = [keep.tile([P, CHUNK, PACK], BF16, name=f"h_grouped{c}", align_bytes=64) for c in range(S // CHUNK)]
+
+        def hidden(b):
+            bank = psum_h.tile([P, PACK, BANK_TOKENS], F32, name="h_bank")
+            codes, plane = x_operand(b * BANK_TOKENS, BANK_TOKENS)
+            for t in range(PACK):
+                cols = slice(t * P, (t + 1) * P)
+                nc.tensor.matmul_mx(
+                    bank[:, t, :], w2_codes[:, cols].bitcast(FP8X4), w2_plane[:, cols], codes, plane, start=True, stop=True
+                )
+            c, lo = divmod(b * BANK_TOKENS, CHUNK)
+            dst = h_grouped[c][:, lo : lo + BANK_TOKENS, :]
+            src = bank[:].rearrange("p t n -> p n t")
+            if b in VECTOR_H_BANKS:
+                nc.vector.tensor_scalar_max(dst, src, 0.0)
+            else:
+                nc.scalar.activation(dst, src, RELU)
+
+        out_rows = out.rearrange("(u p) s -> p u s", p=P)
+
+        def output(c, h_codes, h_plane):
+            bank = psum_o.tile([P, N // P, CHUNK], F32, name="o_bank")
+            codes, plane = x_operand(c * CHUNK, CHUNK)
+            for u in range(N // P):
+                cols = slice(u * P, (u + 1) * P)
+                nc.tensor.matmul_mx(
+                    bank[:, u, :], w1_codes[:, cols].bitcast(FP8X4), w1_plane[:, cols], codes, plane, start=True, stop=False
+                )
+                nc.tensor.matmul_mx(
+                    bank[:, u, :], w3_codes[:, cols].bitcast(FP8X4), w3_plane[:, cols],
+                    h_codes[:].bitcast(FP8X4), h_plane[:], start=False, stop=True,
+                )
+            staged = keep.tile([P, N // P, CHUNK], F32, name=f"staged{c}")
+            if c in VECTOR_OUT_CHUNKS:
+                nc.vector.tensor_copy(staged[:], bank[:])
+            else:
+                nc.scalar.copy(staged[:], bank[:])
+            nc.sync.dma_start(out_rows[:, :, c * CHUNK : (c + 1) * CHUNK], staged[:])
+
+        for b in range(4):
+            hidden(b)
+        w3_grouped = cast_plain(w3_raw, "w3_grouped")
+        w1_grouped = cast_plain(w1_raw, "w1_grouped")
+        w3_codes, w3_plane = quantize(w3_grouped, N, "w3")
+        w1_codes, w1_plane = quantize(w1_grouped, N, "w1")
+        h_q = [quantize(h_grouped[c], CHUNK, f"h{c}") for c in range(2)]
+        for b in range(4, 8):
+            hidden(b)
+        output(0, *h_q[0])
+        h_q.append(quantize(h_grouped[2], CHUNK, "h2"))
+        output(1, *h_q[1])
+        h_q.append(quantize(h_grouped[3], CHUNK, "h3"))
+        output(2, *h_q[2])
+        output(3, *h_q[3])

@@ -18,27 +18,29 @@ P = 128
 PACK = 4
 GATHER = 512
 BANK_TOKENS = 128
-CHUNK = 256
-VECTOR_H_BANKS = (5, 7)
-VECTOR_OUT_CHUNKS = (2,)
+CHUNKS = ((0, 256), (256, 256), (512, 256), (768, 256))
+HEAD = 1024
+VECTOR_H_BANKS = (1, 5, 7)
+VECTOR_OUT_CHUNKS = ()
+WARM = 3
 
 
 def tile_picked_lora_relu_p_kernel(tc, x_words, x_scales, w1, w2, w3, offs, out):
     nc = tc.nc
     with ExitStack() as ctx:
         keep = ctx.enter_context(tc.tile_pool(name="keep", bufs=1))
-        psum_h = ctx.enter_context(tc.psum_pool(name="psum_h", bufs=4))
-        psum_o = ctx.enter_context(tc.psum_pool(name="psum_o", bufs=4))
-
-        offsets = keep.tile([P, S // 16], U16, name="offsets")
-        nc.sync.dma_start(offsets[:], offs)
+        psum = ctx.enter_context(tc.psum_pool(name="psum", bufs=8))
 
         scale_table = keep.tile([P, T], U8, name="scale_table", align_bytes=64)
-        nc.sync.dma_start(scale_table[P - 16 : P, :].bitcast(I32), x_scales[0].bitcast(I32))
-        nc.vector.memset(scale_table[0 : P - 16, :].bitcast(I32), 0)
+        nc.vector.memset(scale_table[:].bitcast(I32), 0)
 
         word_table = keep.tile([P, T], I32, name="word_table", align_bytes=64)
-        nc.sync.dma_start(word_table[:], x_words[0].rearrange("p n t -> p (n t)").bitcast(I32))
+        words_hbm = x_words[0].rearrange("p n t -> p (n t)").bitcast(I32)
+        nc.sync.dma_start(word_table[:, :HEAD], words_hbm[:, :HEAD])
+        offsets = keep.tile([P, S // 16], U16, name="offsets")
+        nc.sync.dma_start(offsets[:], offs)
+        nc.sync.dma_start(scale_table[0:P:8, :].bitcast(I32), x_scales[0].bitcast(I32))
+        nc.sync.dma_start(word_table[:, HEAD:], words_hbm[:, HEAD:])
 
         w2_rows = w2.rearrange("(p j) c -> p j c", j=PACK)
         w2_raw = []
@@ -54,9 +56,9 @@ def tile_picked_lora_relu_p_kernel(tc, x_words, x_scales, w1, w2, w3, offs, out)
         picked_bytes = keep.tile([P, S], U8, name="picked_bytes", align_bytes=64)
         nc.vector.tensor_copy(picked_bytes[:], scale_table[:].indirect(offsets[:]))
         x_plane = keep.tile([P, S], U8, name="x_plane", align_bytes=64)
-        nc.vector.memset(x_plane[:].bitcast(I32), 0)
-        for r in range(4):
-            nc.scalar.dma_start(x_plane[r:P:32, :].bitcast(I32), picked_bytes[P - 16 + r : P : 4, :].bitcast(I32))
+        nc.vector.tensor_copy(x_plane[:].bitcast(I32), picked_bytes[:].bitcast(I32))
+        for r in range(1, 4):
+            nc.scalar.dma_start(x_plane[r:P:32, :].bitcast(I32), picked_bytes[8 * r : P : 32, :].bitcast(I32))
 
         x_codes = []
         for g in range(S // GATHER):
@@ -64,6 +66,13 @@ def tile_picked_lora_relu_p_kernel(tc, x_words, x_scales, w1, w2, w3, offs, out)
             cols = slice(g * GATHER // 16, (g + 1) * GATHER // 16)
             nc.vector.tensor_copy(codes[:], word_table[:].bitcast(U32).indirect(offsets[:, cols]))
             x_codes.append(codes)
+
+        warm_bank = psum.tile([P, GATHER], F32, name="bank")
+        for i in range(WARM):
+            nc.tensor.matmul_mx(
+                warm_bank[:], x_codes[0][:, :P].bitcast(FP8X4), picked_bytes[:, :P],
+                x_codes[0][:].bitcast(FP8X4), picked_bytes[:, :GATHER], start=True, stop=True,
+            )
 
         def x_operand(first, count):
             g, lo = divmod(first, GATHER)
@@ -79,74 +88,115 @@ def tile_picked_lora_relu_p_kernel(tc, x_words, x_scales, w1, w2, w3, offs, out)
         cast_w2(nc.scalar.copy, 0, 0, 64)
         cast_w2(nc.vector.tensor_copy, 1, 0, 40)
         cast_w2(nc.scalar.copy, 1, 40, 64)
-        w2_codes = keep.tile([P, H], U32, name="w2_codes", align_bytes=64)
-        w2_plane = keep.tile([P, H], U8, name="w2_plane", align_bytes=64)
-        nc.vector.quantize_mx(w2_codes[:].bitcast(FP8X4), w2_plane[:], w2_grouped[:].rearrange("p t m j -> p (t m j)"))
 
-        def cast_plain(raw, name):
-            grouped = keep.tile([P, N, PACK], BF16, name=name, align_bytes=64)
-            nc.vector.tensor_copy(
-                grouped[:].rearrange("p (c i) j -> p c j i", i=4), raw[:].rearrange("p j (c i) -> p c j i", i=4)
+        def cast_plain(engine_copy, grouped, raw, lo, hi):
+            engine_copy(
+                grouped[:, lo:hi, :].rearrange("p (c i) j -> p c j i", i=4),
+                raw[:, :, lo:hi].rearrange("p j (c i) -> p c j i", i=4),
             )
-            return grouped
 
-        def quantize(grouped, width, name):
+        w3_grouped = keep.tile([P, N, PACK], BF16, name="w3_grouped", align_bytes=64)
+        w1_grouped = keep.tile([P, N, PACK], BF16, name="w1_grouped", align_bytes=64)
+
+        def quantize(grouped, name):
+            width = grouped.shape[1]
             codes = keep.tile([P, width], U32, name=name + "_codes", align_bytes=64)
             plane = keep.tile([P, width], U8, name=name + "_plane", align_bytes=64)
-            nc.vector.quantize_mx(codes[:].bitcast(FP8X4), plane[:], grouped[:].rearrange("p c j -> p (c j)"))
+            nc.vector.quantize_mx(codes[:].bitcast(FP8X4), plane[:], grouped.rearrange("p c j -> p (c j)"))
             return codes, plane
 
-        h_grouped = [keep.tile([P, CHUNK, PACK], BF16, name=f"h_grouped{c}", align_bytes=64) for c in range(S // CHUNK)]
+        w2_q = [quantize(w2_grouped[:, t], f"w2_{t}") for t in range(PACK)]
 
-        def hidden(b):
-            bank = psum_h.tile([P, PACK, BANK_TOKENS], F32, name="h_bank")
+        h_grouped = keep.tile([P, S, PACK], BF16, name="h_grouped", align_bytes=64)
+
+        def hidden_pass(bank, b, t):
             codes, plane = x_operand(b * BANK_TOKENS, BANK_TOKENS)
-            for t in range(PACK):
-                cols = slice(t * P, (t + 1) * P)
-                nc.tensor.matmul_mx(
-                    bank[:, t, :], w2_codes[:, cols].bitcast(FP8X4), w2_plane[:, cols], codes, plane, start=True, stop=True
-                )
-            c, lo = divmod(b * BANK_TOKENS, CHUNK)
-            dst = h_grouped[c][:, lo : lo + BANK_TOKENS, :]
+            nc.tensor.matmul_mx(bank[:, t, :], w2_q[t][0][:].bitcast(FP8X4), w2_q[t][1][:], codes, plane, start=True, stop=True)
+
+        def relu_out(bank, b):
+            dst = h_grouped[:, b * BANK_TOKENS : (b + 1) * BANK_TOKENS, :]
             src = bank[:].rearrange("p t n -> p n t")
             if b in VECTOR_H_BANKS:
                 nc.vector.tensor_scalar_max(dst, src, 0.0)
             else:
                 nc.scalar.activation(dst, src, RELU)
 
+        def new_h_bank():
+            return psum.tile([P, PACK, BANK_TOKENS], F32, name="bank")
+
+        def hidden(b):
+            bank = new_h_bank()
+            for t in range(PACK):
+                hidden_pass(bank, b, t)
+            relu_out(bank, b)
+
+        def quantize_h(c):
+            first, count = CHUNKS[c]
+            return quantize(h_grouped[:, first : first + count, :], f"h{c}")
+
         out_rows = out.rearrange("(u p) s -> p u s", p=P)
 
+        def own_pass(dst, c, u):
+            codes, plane = x_operand(*CHUNKS[c])
+            cols = slice(u * P, (u + 1) * P)
+            nc.tensor.matmul_mx(dst, w1_codes[:, cols].bitcast(FP8X4), w1_plane[:, cols], codes, plane, start=True, stop=False)
+
+        def adapter_pass(dst, u, h_codes, h_plane):
+            cols = slice(u * P, (u + 1) * P)
+            nc.tensor.matmul_mx(
+                dst, w3_codes[:, cols].bitcast(FP8X4), w3_plane[:, cols],
+                h_codes[:].bitcast(FP8X4), h_plane[:], start=False, stop=True,
+            )
+
         def output(c, h_codes, h_plane):
-            bank = psum_o.tile([P, N // P, CHUNK], F32, name="o_bank")
-            codes, plane = x_operand(c * CHUNK, CHUNK)
+            first, count = CHUNKS[c]
+            bank = psum.tile([P, N // P, count], F32, name="bank")
             for u in range(N // P):
-                cols = slice(u * P, (u + 1) * P)
-                nc.tensor.matmul_mx(
-                    bank[:, u, :], w1_codes[:, cols].bitcast(FP8X4), w1_plane[:, cols], codes, plane, start=True, stop=False
-                )
-                nc.tensor.matmul_mx(
-                    bank[:, u, :], w3_codes[:, cols].bitcast(FP8X4), w3_plane[:, cols],
-                    h_codes[:].bitcast(FP8X4), h_plane[:], start=False, stop=True,
-                )
-            staged = keep.tile([P, N // P, CHUNK], F32, name=f"staged{c}")
+                own_pass(bank[:, u, :], c, u)
+                adapter_pass(bank[:, u, :], u, h_codes, h_plane)
+            staged = keep.tile([P, N // P, count], F32, name=f"staged{c}")
             if c in VECTOR_OUT_CHUNKS:
                 nc.vector.tensor_copy(staged[:], bank[:])
             else:
                 nc.scalar.copy(staged[:], bank[:])
-            nc.sync.dma_start(out_rows[:, :, c * CHUNK : (c + 1) * CHUNK], staged[:])
+            nc.sync.dma_start(out_rows[:, :, first : first + count], staged[:])
 
+        def open_split(c):
+            banks = [psum.tile([P, CHUNKS[c][1]], F32, name="bank") for u in range(N // P)]
+            for u in range(N // P):
+                own_pass(banks[u][:], c, u)
+            return banks
+
+        def close_split(c, banks, h_codes, h_plane):
+            first, count = CHUNKS[c]
+            for u, engine_copy in enumerate((nc.scalar.copy, nc.vector.tensor_copy)):
+                adapter_pass(banks[u][:], u, h_codes, h_plane)
+                staged = keep.tile([P, count], F32, name=f"staged{c}_{u}")
+                engine_copy(staged[:], banks[u][:])
+                nc.sync.dma_start(out_rows[:, u, first : first + count], staged[:])
+
+        first_banks = [new_h_bank() for b in range(4)]
+        for t in range(PACK):
+            for b in range(4):
+                hidden_pass(first_banks[b], b, t)
+        cast_plain(nc.scalar.copy, w3_grouped, w3_raw, 0, 128)
+        cast_plain(nc.vector.tensor_copy, w3_grouped, w3_raw, 128, 256)
+        w3_codes, w3_plane = quantize(w3_grouped[:], "w3")
+        cast_plain(nc.vector.tensor_copy, w1_grouped, w1_raw, 0, 256)
         for b in range(4):
-            hidden(b)
-        w3_grouped = cast_plain(w3_raw, "w3_grouped")
-        w1_grouped = cast_plain(w1_raw, "w1_grouped")
-        w3_codes, w3_plane = quantize(w3_grouped, N, "w3")
-        w1_codes, w1_plane = quantize(w1_grouped, N, "w1")
-        h_q = [quantize(h_grouped[c], CHUNK, f"h{c}") for c in range(2)]
-        for b in range(4, 8):
-            hidden(b)
-        output(0, *h_q[0])
-        h_q.append(quantize(h_grouped[2], CHUNK, "h2"))
-        output(1, *h_q[1])
-        h_q.append(quantize(h_grouped[3], CHUNK, "h3"))
-        output(2, *h_q[2])
-        output(3, *h_q[3])
+            relu_out(first_banks[b], b)
+        w1_codes, w1_plane = quantize(w1_grouped[:], "w1")
+        h0 = quantize_h(0)
+        hidden(4)
+        hidden(5)
+        h1 = quantize_h(1)
+        hidden(6)
+        hidden(7)
+        output(0, *h0)
+        output(1, *h1)
+        banks2 = open_split(2)
+        banks3 = open_split(3)
+        h2 = quantize_h(2)
+        h3 = quantize_h(3)
+        close_split(2, banks2, *h2)
+        close_split(3, banks3, *h3)

@@ -18,10 +18,10 @@ P = 128
 PACK = 4
 GATHER = 512
 BANK_TOKENS = 128
-CHUNKS = ((0, 256), (256, 256), (512, 256), (768, 256))
+CHUNKS = ((0, 256), (256, 256), (512, 256), (768, 128), (896, 128))
 HEAD = 1024
 VECTOR_H_BANKS = (1, 5, 7)
-VECTOR_OUT_CHUNKS = ()
+VECTOR_OUT_CHUNKS = (3,)
 WARM = 3
 
 
@@ -52,6 +52,10 @@ def tile_picked_lora_relu_p_kernel(tc, x_words, x_scales, w1, w2, w3, offs, out)
         nc.sync.dma_start(w3_raw[:], w3.rearrange("(p j) c -> p j c", j=PACK))
         w1_raw = keep.tile([P, PACK, N], F32, name="w1_raw")
         nc.sync.dma_start(w1_raw[:], w1.rearrange("(p j) c -> p j c", j=PACK))
+
+        table_warm = keep.tile([P, 8], F32, name="table_warm")
+        nc.gpsimd.memset(table_warm[:], 0.0)
+        nc.scalar.activation(table_warm[:], table_warm[:], RELU)
 
         picked_bytes = keep.tile([P, S], U8, name="picked_bytes", align_bytes=64)
         nc.vector.tensor_copy(picked_bytes[:], scale_table[:].indirect(offsets[:]))
@@ -105,13 +109,15 @@ def tile_picked_lora_relu_p_kernel(tc, x_words, x_scales, w1, w2, w3, offs, out)
             nc.vector.quantize_mx(codes[:].bitcast(FP8X4), plane[:], grouped.rearrange("p c j -> p (c j)"))
             return codes, plane
 
-        w2_q = [quantize(w2_grouped[:, t], f"w2_{t}") for t in range(PACK)]
+        w2_q = [quantize(w2_grouped[:, 2 * i : 2 * i + 2].rearrange("p t m j -> p (t m) j"), f"w2_{i}") for i in range(2)]
 
         h_grouped = keep.tile([P, S, PACK], BF16, name="h_grouped", align_bytes=64)
 
         def hidden_pass(bank, b, t):
             codes, plane = x_operand(b * BANK_TOKENS, BANK_TOKENS)
-            nc.tensor.matmul_mx(bank[:, t, :], w2_q[t][0][:].bitcast(FP8X4), w2_q[t][1][:], codes, plane, start=True, stop=True)
+            w2_codes, w2_plane = w2_q[t // 2]
+            cols = slice((t % 2) * P, (t % 2 + 1) * P)
+            nc.tensor.matmul_mx(bank[:, t, :], w2_codes[:, cols].bitcast(FP8X4), w2_plane[:, cols], codes, plane, start=True, stop=True)
 
         def relu_out(bank, b):
             dst = h_grouped[:, b * BANK_TOKENS : (b + 1) * BANK_TOKENS, :]
@@ -169,16 +175,17 @@ def tile_picked_lora_relu_p_kernel(tc, x_words, x_scales, w1, w2, w3, offs, out)
 
         def close_split(c, banks, h_codes, h_plane):
             first, count = CHUNKS[c]
+            staged = keep.tile([P, N // P, count], F32, name=f"staged{c}")
             for u, engine_copy in enumerate((nc.scalar.copy, nc.vector.tensor_copy)):
                 adapter_pass(banks[u][:], u, h_codes, h_plane)
-                staged = keep.tile([P, count], F32, name=f"staged{c}_{u}")
-                engine_copy(staged[:], banks[u][:])
-                nc.sync.dma_start(out_rows[:, u, first : first + count], staged[:])
+                engine_copy(staged[:, u, :], banks[u][:])
+            nc.sync.dma_start(out_rows[:, :, first : first + count], staged[:])
 
         first_banks = [new_h_bank() for b in range(4)]
-        for t in range(PACK):
+        for pair in range(2):
             for b in range(4):
-                hidden_pass(first_banks[b], b, t)
+                hidden_pass(first_banks[b], b, 2 * pair)
+                hidden_pass(first_banks[b], b, 2 * pair + 1)
         cast_plain(nc.scalar.copy, w3_grouped, w3_raw, 0, 128)
         cast_plain(nc.vector.tensor_copy, w3_grouped, w3_raw, 128, 256)
         w3_codes, w3_plane = quantize(w3_grouped[:], "w3")
@@ -189,14 +196,14 @@ def tile_picked_lora_relu_p_kernel(tc, x_words, x_scales, w1, w2, w3, offs, out)
         h0 = quantize_h(0)
         hidden(4)
         hidden(5)
+        output(0, *h0)
         h1 = quantize_h(1)
         hidden(6)
         hidden(7)
-        output(0, *h0)
         output(1, *h1)
-        banks2 = open_split(2)
-        banks3 = open_split(3)
         h2 = quantize_h(2)
         h3 = quantize_h(3)
-        close_split(2, banks2, *h2)
-        close_split(3, banks3, *h3)
+        h4 = quantize_h(4)
+        output(2, *h2)
+        output(3, *h3)
+        output(4, *h4)

@@ -39,7 +39,8 @@ def tile_picked_lora_relu_p_kernel(tc, x_words, x_scales, w1, w2, w3, offs, out)
         nc.sync.dma_start(word_table[:, :HEAD], words_hbm[:, :HEAD])
         offsets = keep.tile([P, S // 16], U16, name="offsets")
         nc.sync.dma_start(offsets[:], offs)
-        nc.sync.dma_start(scale_table[0:P:8, :].bitcast(I32), x_scales[0].bitcast(I32))
+        for r in range(4):
+            nc.sync.dma_start(scale_table[r:P:32, :].bitcast(I32), x_scales[0, r:16:4, :].bitcast(I32))
         nc.sync.dma_start(word_table[:, HEAD:], words_hbm[:, HEAD:])
 
         w2_rows = w2.rearrange("(p j) c -> p j c", j=PACK)
@@ -53,16 +54,9 @@ def tile_picked_lora_relu_p_kernel(tc, x_words, x_scales, w1, w2, w3, offs, out)
         w1_raw = keep.tile([P, PACK, N], F32, name="w1_raw")
         nc.sync.dma_start(w1_raw[:], w1.rearrange("(p j) c -> p j c", j=PACK))
 
-        table_warm = keep.tile([P, 8], F32, name="table_warm")
-        nc.gpsimd.memset(table_warm[:], 0.0)
-        nc.scalar.activation(table_warm[:], table_warm[:], RELU)
-
         picked_bytes = keep.tile([P, S], U8, name="picked_bytes", align_bytes=64)
         nc.vector.tensor_copy(picked_bytes[:], scale_table[:].indirect(offsets[:]))
-        x_plane = keep.tile([P, S], U8, name="x_plane", align_bytes=64)
-        nc.vector.tensor_copy(x_plane[:].bitcast(I32), picked_bytes[:].bitcast(I32))
-        for r in range(1, 4):
-            nc.scalar.dma_start(x_plane[r:P:32, :].bitcast(I32), picked_bytes[8 * r : P : 32, :].bitcast(I32))
+        x_plane = picked_bytes
 
         x_codes = []
         for g in range(S // GATHER):

@@ -19,9 +19,9 @@ PACK = 4
 GATHER = 512
 BANK_TOKENS = 128
 CHUNKS = ((0, 256), (256, 256), (512, 256), (768, 128), (896, 128))
-HEAD = 1024
-VECTOR_H_BANKS = (1, 5, 7)
-VECTOR_OUT_CHUNKS = (3,)
+W2_VECTOR_EXTRA = 16
+W1_SCALAR = 64
+W3_SCALAR = 80
 WARM = 3
 
 
@@ -29,34 +29,33 @@ def tile_picked_lora_relu_p_kernel(tc, x_words, x_scales, w1, w2, w3, offs, out)
     nc = tc.nc
     with ExitStack() as ctx:
         keep = ctx.enter_context(tc.tile_pool(name="keep", bufs=1))
-        psum = ctx.enter_context(tc.psum_pool(name="psum", bufs=8))
+        psum = ctx.enter_context(tc.psum_pool(name="psum", bufs=1))
 
         scale_table = keep.tile([P, T], U8, name="scale_table", align_bytes=64)
-        nc.vector.memset(scale_table[:].bitcast(I32), 0)
+        nc.vector.memset(scale_table[: P - 16, :].bitcast(I32), 0)
+        x_plane = keep.tile([P, S], U8, name="x_plane", align_bytes=64)
+        nc.gpsimd.memset(x_plane[:].bitcast(I32), 0)
 
         word_table = keep.tile([P, T], I32, name="word_table", align_bytes=64)
         words_hbm = x_words[0].rearrange("p n t -> p (n t)").bitcast(I32)
-        nc.sync.dma_start(word_table[:, :HEAD], words_hbm[:, :HEAD])
         offsets = keep.tile([P, S // 16], U16, name="offsets")
         nc.sync.dma_start(offsets[:], offs)
-        for r in range(4):
-            nc.sync.dma_start(scale_table[r:P:32, :].bitcast(I32), x_scales[0, r:16:4, :].bitcast(I32))
-        nc.sync.dma_start(word_table[:, HEAD:], words_hbm[:, HEAD:])
-
-        w2_rows = w2.rearrange("(p j) c -> p j c", j=PACK)
-        w2_raw = []
-        for half in range(2):
-            raw = keep.tile([P, PACK, H // 2], F32, name=f"w2_raw{half}")
-            nc.sync.dma_start(raw[:], w2_rows[:, :, half * (H // 2) : (half + 1) * (H // 2)])
-            w2_raw.append(raw)
-        w3_raw = keep.tile([P, PACK, N], F32, name="w3_raw")
-        nc.sync.dma_start(w3_raw[:], w3.rearrange("(p j) c -> p j c", j=PACK))
-        w1_raw = keep.tile([P, PACK, N], F32, name="w1_raw")
-        nc.sync.dma_start(w1_raw[:], w1.rearrange("(p j) c -> p j c", j=PACK))
+        nc.sync.dma_start(scale_table[P - 16 :, :].bitcast(I32), x_scales[0].bitcast(I32))
+        nc.sync.dma_start(word_table[:], words_hbm)
 
         picked_bytes = keep.tile([P, S], U8, name="picked_bytes", align_bytes=64)
         nc.vector.tensor_copy(picked_bytes[:], scale_table[:].indirect(offsets[:]))
-        x_plane = picked_bytes
+
+        w2_rows = w2.rearrange("(p j) c -> p j c", j=PACK)
+        w2_raw = [keep.tile([P, PACK, H // 2], F32, name=f"w2_raw{half}") for half in range(2)]
+        nc.sync.dma_start(w2_raw[0][:], w2_rows[:, :, : H // 2])
+        for q in range(4):
+            nc.sync.dma_start(x_plane[32 * q : 32 * q + 4, :].bitcast(I32), picked_bytes[P - 16 + 4 * q : P - 12 + 4 * q, :].bitcast(I32))
+        nc.sync.dma_start(w2_raw[1][:], w2_rows[:, :, H // 2 :])
+        w1_raw = keep.tile([P, PACK, N], F32, name="w1_raw")
+        nc.sync.dma_start(w1_raw[:], w1.rearrange("(p j) c -> p j c", j=PACK))
+        w3_raw = keep.tile([P, PACK, N], F32, name="w3_raw")
+        nc.sync.dma_start(w3_raw[:], w3.rearrange("(p j) c -> p j c", j=PACK))
 
         x_codes = []
         for g in range(S // GATHER):
@@ -65,7 +64,10 @@ def tile_picked_lora_relu_p_kernel(tc, x_words, x_scales, w1, w2, w3, offs, out)
             nc.vector.tensor_copy(codes[:], word_table[:].bitcast(U32).indirect(offsets[:, cols]))
             x_codes.append(codes)
 
-        warm_bank = psum.tile([P, GATHER], F32, name="bank")
+        def bank_tile(bank, shape):
+            return psum.tile([P] + shape, F32, name=f"bank{bank}")
+
+        warm_bank = bank_tile(7, [GATHER])
         for i in range(WARM):
             nc.tensor.matmul_mx(
                 warm_bank[:], x_codes[0][:, :P].bitcast(FP8X4), picked_bytes[:, :P],
@@ -76,16 +78,12 @@ def tile_picked_lora_relu_p_kernel(tc, x_words, x_scales, w1, w2, w3, offs, out)
             g, lo = divmod(first, GATHER)
             return x_codes[g][:, lo : lo + count].bitcast(FP8X4), x_plane[:, first : first + count]
 
-        w2_grouped = keep.tile([P, PACK, P, PACK], BF16, name="w2_grouped", align_bytes=64)
+        w2_grouped = [keep.tile([P, 2, P, PACK], BF16, name=f"w2_grouped{i}", align_bytes=64) for i in range(2)]
 
-        def cast_w2(engine_copy, half, lo, hi):
-            dst = w2_grouped[:, :, half * 64 + lo : half * 64 + hi, :].rearrange("p t m j -> p m t j")
+        def cast_w2(engine_copy, half, pair, lo, hi):
+            dst = w2_grouped[pair][:, :, half * 64 + lo : half * 64 + hi, :].rearrange("p t m j -> p m t j")
             src = w2_raw[half][:, :, lo * PACK : hi * PACK].rearrange("p j (m t) -> p m t j", t=PACK)
-            engine_copy(dst, src)
-
-        cast_w2(nc.scalar.copy, 0, 0, 64)
-        cast_w2(nc.vector.tensor_copy, 1, 0, 40)
-        cast_w2(nc.scalar.copy, 1, 40, 64)
+            engine_copy(dst, src[:, :, 2 * pair : 2 * pair + 2, :])
 
         def cast_plain(engine_copy, grouped, raw, lo, hi):
             engine_copy(
@@ -103,32 +101,33 @@ def tile_picked_lora_relu_p_kernel(tc, x_words, x_scales, w1, w2, w3, offs, out)
             nc.vector.quantize_mx(codes[:].bitcast(FP8X4), plane[:], grouped.rearrange("p c j -> p (c j)"))
             return codes, plane
 
-        w2_q = [quantize(w2_grouped[:, 2 * i : 2 * i + 2].rearrange("p t m j -> p (t m) j"), f"w2_{i}") for i in range(2)]
+        cast_w2(nc.scalar.copy, 0, 0, 0, 64)
+        cast_w2(nc.scalar.copy, 0, 1, 0, 64)
+        cast_w2(nc.vector.tensor_copy, 1, 0, 0, 64)
+        cast_w2(nc.vector.tensor_copy, 1, 1, 0, W2_VECTOR_EXTRA)
+        cast_w2(nc.scalar.copy, 1, 1, W2_VECTOR_EXTRA, 64)
+        w2_q = [quantize(w2_grouped[i][:].rearrange("p t m j -> p (t m) j"), f"w2_{i}") for i in range(2)]
 
         h_grouped = keep.tile([P, S, PACK], BF16, name="h_grouped", align_bytes=64)
+        h_banks = [bank_tile(b, [PACK, BANK_TOKENS]) for b in range(S // BANK_TOKENS)]
 
-        def hidden_pass(bank, b, t):
+        def hidden_pair(b, pair):
             codes, plane = x_operand(b * BANK_TOKENS, BANK_TOKENS)
-            w2_codes, w2_plane = w2_q[t // 2]
-            cols = slice((t % 2) * P, (t % 2 + 1) * P)
-            nc.tensor.matmul_mx(bank[:, t, :], w2_codes[:, cols].bitcast(FP8X4), w2_plane[:, cols], codes, plane, start=True, stop=True)
+            w2_codes, w2_plane = w2_q[pair]
+            for e in range(2):
+                cols = slice(e * P, (e + 1) * P)
+                nc.tensor.matmul_mx(
+                    h_banks[b][:, 2 * pair + e, :], w2_codes[:, cols].bitcast(FP8X4), w2_plane[:, cols],
+                    codes, plane, start=True, stop=True,
+                )
 
-        def relu_out(bank, b):
+        def relu_out(b, on_vector):
             dst = h_grouped[:, b * BANK_TOKENS : (b + 1) * BANK_TOKENS, :]
-            src = bank[:].rearrange("p t n -> p n t")
-            if b in VECTOR_H_BANKS:
+            src = h_banks[b][:].rearrange("p t n -> p n t")
+            if on_vector:
                 nc.vector.tensor_scalar_max(dst, src, 0.0)
             else:
                 nc.scalar.activation(dst, src, RELU)
-
-        def new_h_bank():
-            return psum.tile([P, PACK, BANK_TOKENS], F32, name="bank")
-
-        def hidden(b):
-            bank = new_h_bank()
-            for t in range(PACK):
-                hidden_pass(bank, b, t)
-            relu_out(bank, b)
 
         def quantize_h(c):
             first, count = CHUNKS[c]
@@ -141,63 +140,71 @@ def tile_picked_lora_relu_p_kernel(tc, x_words, x_scales, w1, w2, w3, offs, out)
             cols = slice(u * P, (u + 1) * P)
             nc.tensor.matmul_mx(dst, w1_codes[:, cols].bitcast(FP8X4), w1_plane[:, cols], codes, plane, start=True, stop=False)
 
-        def adapter_pass(dst, u, h_codes, h_plane):
+        def adapter_pass(dst, u, h_q):
             cols = slice(u * P, (u + 1) * P)
             nc.tensor.matmul_mx(
                 dst, w3_codes[:, cols].bitcast(FP8X4), w3_plane[:, cols],
-                h_codes[:].bitcast(FP8X4), h_plane[:], start=False, stop=True,
+                h_q[0][:].bitcast(FP8X4), h_q[1][:], start=False, stop=True,
             )
 
-        def output(c, h_codes, h_plane):
-            first, count = CHUNKS[c]
-            bank = psum.tile([P, N // P, count], F32, name="bank")
+        def open_chunk(c, banks):
+            tiles = [bank_tile(bank, [CHUNKS[c][1]]) for bank in banks]
             for u in range(N // P):
-                own_pass(bank[:, u, :], c, u)
-                adapter_pass(bank[:, u, :], u, h_codes, h_plane)
-            staged = keep.tile([P, N // P, count], F32, name=f"staged{c}")
-            if c in VECTOR_OUT_CHUNKS:
-                nc.vector.tensor_copy(staged[:], bank[:])
-            else:
-                nc.scalar.copy(staged[:], bank[:])
-            nc.sync.dma_start(out_rows[:, :, first : first + count], staged[:])
+                own_pass(tiles[u][:], c, u)
+            return tiles
 
-        def open_split(c):
-            banks = [psum.tile([P, CHUNKS[c][1]], F32, name="bank") for u in range(N // P)]
+        def close_chunk(tiles, h_q):
             for u in range(N // P):
-                own_pass(banks[u][:], c, u)
-            return banks
+                adapter_pass(tiles[u][:], u, h_q)
 
-        def close_split(c, banks, h_codes, h_plane):
+        def store_chunk(c, tiles, copies):
             first, count = CHUNKS[c]
             staged = keep.tile([P, N // P, count], F32, name=f"staged{c}")
-            for u, engine_copy in enumerate((nc.scalar.copy, nc.vector.tensor_copy)):
-                adapter_pass(banks[u][:], u, h_codes, h_plane)
-                engine_copy(staged[:, u, :], banks[u][:])
+            for u in range(N // P):
+                copies[u](staged[:, u, :], tiles[u][:])
             nc.sync.dma_start(out_rows[:, :, first : first + count], staged[:])
 
-        first_banks = [new_h_bank() for b in range(4)]
+        on_scalar = (nc.scalar.copy, nc.scalar.copy)
+        on_both = (nc.vector.tensor_copy, nc.scalar.copy)
+
         for pair in range(2):
-            for b in range(4):
-                hidden_pass(first_banks[b], b, 2 * pair)
-                hidden_pass(first_banks[b], b, 2 * pair + 1)
-        cast_plain(nc.scalar.copy, w3_grouped, w3_raw, 0, 128)
-        cast_plain(nc.vector.tensor_copy, w3_grouped, w3_raw, 128, 256)
-        w3_codes, w3_plane = quantize(w3_grouped[:], "w3")
-        cast_plain(nc.vector.tensor_copy, w1_grouped, w1_raw, 0, 256)
-        for b in range(4):
-            relu_out(first_banks[b], b)
+            for b in range(2):
+                hidden_pair(b, pair)
+        for b in range(2, 8):
+            for pair in range(2):
+                hidden_pair(b, pair)
+
+        cast_plain(nc.scalar.copy, w1_grouped, w1_raw, 0, W1_SCALAR)
+        cast_plain(nc.vector.tensor_copy, w1_grouped, w1_raw, W1_SCALAR, N)
+        relu_out(0, False)
+        relu_out(1, True)
+        relu_out(2, False)
         w1_codes, w1_plane = quantize(w1_grouped[:], "w1")
+        cast_plain(nc.vector.tensor_copy, w3_grouped, w3_raw, W3_SCALAR, N)
+        cast_plain(nc.scalar.copy, w3_grouped, w3_raw, 0, W3_SCALAR)
         h0 = quantize_h(0)
-        hidden(4)
-        hidden(5)
-        output(0, *h0)
+        relu_out(3, False)
+        w3_codes, w3_plane = quantize(w3_grouped[:], "w3")
+        out0 = open_chunk(0, (0, 1))
+        close_chunk(out0, h0)
+        out1 = open_chunk(1, (2, 3))
+        relu_out(4, False)
         h1 = quantize_h(1)
-        hidden(6)
-        hidden(7)
-        output(1, *h1)
+        close_chunk(out1, h1)
+        relu_out(5, True)
+        store_chunk(0, out0, on_scalar)
+        out2 = open_chunk(2, (4, 5))
+        relu_out(6, True)
+        store_chunk(1, out1, on_scalar)
+        out3 = open_chunk(3, (0, 1))
         h2 = quantize_h(2)
+        close_chunk(out2, h2)
+        relu_out(7, False)
         h3 = quantize_h(3)
+        close_chunk(out3, h3)
+        out4 = open_chunk(4, (2, 3))
+        store_chunk(2, out2, on_both)
         h4 = quantize_h(4)
-        output(2, *h2)
-        output(3, *h3)
-        output(4, *h4)
+        close_chunk(out4, h4)
+        store_chunk(3, out3, on_scalar)
+        store_chunk(4, out4, on_both)

@@ -81,9 +81,9 @@ def tile_picked_lora_relu_p_kernel(tc, x_words, x_scales, w1, w2, w3, offs, out)
         w2_grouped = [keep.tile([P, 2, P, PACK], BF16, name=f"w2_grouped{i}", align_bytes=64) for i in range(2)]
 
         def cast_w2(engine_copy, half, pair, lo, hi):
-            dst = w2_grouped[pair][:, :, half * 64 + lo : half * 64 + hi, :].rearrange("p t m j -> p m t j")
-            src = w2_raw[half][:, :, lo * PACK : hi * PACK].rearrange("p j (m t) -> p m t j", t=PACK)
-            engine_copy(dst, src[:, :, 2 * pair : 2 * pair + 2, :])
+            dst = w2_grouped[pair][:, :, half * 64 + lo : half * 64 + hi, :].rearrange("p t m j -> p m j t")
+            src = w2_raw[half][:, :, lo * PACK : hi * PACK].rearrange("p j (m t) -> p m j t", t=PACK)
+            engine_copy(dst, src[:, :, :, 2 * pair : 2 * pair + 2])
 
         def cast_plain(engine_copy, grouped, raw, lo, hi):
             engine_copy(
@@ -162,7 +162,10 @@ def tile_picked_lora_relu_p_kernel(tc, x_words, x_scales, w1, w2, w3, offs, out)
             staged = keep.tile([P, N // P, count], F32, name=f"staged{c}")
             for u in range(N // P):
                 copies[u](staged[:, u, :], tiles[u][:])
-            nc.sync.dma_start(out_rows[:, :, first : first + count], staged[:])
+                if count == 256:
+                    nc.sync.dma_start(out_rows[:, u, first : first + count], staged[:, u, :])
+            if count < 256:
+                nc.sync.dma_start(out_rows[:, :, first : first + count], staged[:])
 
         on_scalar = (nc.scalar.copy, nc.scalar.copy)
         on_both = (nc.vector.tensor_copy, nc.scalar.copy)
@@ -180,31 +183,30 @@ def tile_picked_lora_relu_p_kernel(tc, x_words, x_scales, w1, w2, w3, offs, out)
         relu_out(1, True)
         relu_out(2, False)
         w1_codes, w1_plane = quantize(w1_grouped[:], "w1")
-        cast_plain(nc.vector.tensor_copy, w3_grouped, w3_raw, W3_SCALAR, N)
-        cast_plain(nc.scalar.copy, w3_grouped, w3_raw, 0, W3_SCALAR)
-        h0 = quantize_h(0)
+        cast_plain(nc.vector.tensor_copy, w3_grouped, w3_raw, 0, N)
         relu_out(3, False)
+        h0 = quantize_h(0)
+        relu_out(4, False)
         w3_codes, w3_plane = quantize(w3_grouped[:], "w3")
         out0 = open_chunk(0, (0, 1))
         close_chunk(out0, h0)
         out1 = open_chunk(1, (2, 3))
-        relu_out(4, False)
+        relu_out(5, False)
         h1 = quantize_h(1)
         close_chunk(out1, h1)
-        relu_out(5, True)
         store_chunk(0, out0, on_scalar)
         out2 = open_chunk(2, (4, 5))
+        h2 = quantize_h(2)
+        close_chunk(out2, h2)
         relu_out(6, True)
         store_chunk(1, out1, on_scalar)
         out3 = open_chunk(3, (0, 1))
-        h2 = quantize_h(2)
-        close_chunk(out2, h2)
-        relu_out(7, False)
+        relu_out(7, True)
         h3 = quantize_h(3)
         close_chunk(out3, h3)
         out4 = open_chunk(4, (2, 3))
-        store_chunk(2, out2, on_both)
+        store_chunk(2, out2, on_scalar)
         h4 = quantize_h(4)
         close_chunk(out4, h4)
-        store_chunk(3, out3, on_scalar)
+        store_chunk(3, out3, on_both)
         store_chunk(4, out4, on_both)

@@ -15,14 +15,16 @@ FP8X4 = mybir.dt.float8_e4m3fn_x4
 RELU = mybir.ActivationFunctionType.Relu
 
 P = 128
-PACK = 4
+SLOTS = 4
+BLOCKS = K // 32
+LIST_ROWS = 16
 GATHER = 512
-BANK_TOKENS = 128
+GROUP = 128
 CHUNKS = ((0, 256), (256, 256), (512, 256), (768, 128), (896, 128))
-W2_VECTOR_EXTRA = 16
-W1_SCALAR = 64
-W3_SCALAR = 80
-WARM = 3
+HALF = P // 2
+W2_VECTOR_GROUPS = 16
+W1_SCALAR_COLUMNS = 64
+WARM_UP_PASSES = 4
 
 
 def tile_picked_lora_relu_p_kernel(tc, x_words, x_scales, w1, w2, w3, offs, out):
@@ -31,44 +33,45 @@ def tile_picked_lora_relu_p_kernel(tc, x_words, x_scales, w1, w2, w3, offs, out)
         keep = ctx.enter_context(tc.tile_pool(name="keep", bufs=1))
         psum = ctx.enter_context(tc.psum_pool(name="psum", bufs=1))
 
+        first_row = P - BLOCKS
         scale_table = keep.tile([P, T], U8, name="scale_table", align_bytes=64)
-        nc.vector.memset(scale_table[: P - 16, :].bitcast(I32), 0)
+        nc.vector.memset(scale_table[:first_row, :].bitcast(I32), 0)
         x_plane = keep.tile([P, S], U8, name="x_plane", align_bytes=64)
         nc.gpsimd.memset(x_plane[:].bitcast(I32), 0)
 
         word_table = keep.tile([P, T], I32, name="word_table", align_bytes=64)
-        words_hbm = x_words[0].rearrange("p n t -> p (n t)").bitcast(I32)
-        offsets = keep.tile([P, S // 16], U16, name="offsets")
+        offsets = keep.tile([P, S // LIST_ROWS], U16, name="offsets")
         nc.sync.dma_start(offsets[:], offs)
-        nc.sync.dma_start(scale_table[P - 16 :, :].bitcast(I32), x_scales[0].bitcast(I32))
-        nc.sync.dma_start(word_table[:], words_hbm)
+        nc.sync.dma_start(scale_table[first_row:, :].bitcast(I32), x_scales[0].bitcast(I32))
+        nc.sync.dma_start(word_table[:], x_words[0].rearrange("p n t -> p (n t)").bitcast(I32))
 
         picked_bytes = keep.tile([P, S], U8, name="picked_bytes", align_bytes=64)
         nc.vector.tensor_copy(picked_bytes[:], scale_table[:].indirect(offsets[:]))
 
-        w2_rows = w2.rearrange("(p j) c -> p j c", j=PACK)
-        w2_raw = [keep.tile([P, PACK, H // 2], F32, name=f"w2_raw{half}") for half in range(2)]
+        w2_rows = w2.rearrange("(p j) c -> p j c", j=SLOTS)
+        w2_raw = [keep.tile([P, SLOTS, H // 2], F32, name=f"w2_raw{half}") for half in range(2)]
         nc.sync.dma_start(w2_raw[0][:], w2_rows[:, :, : H // 2])
         for q in range(4):
-            nc.sync.dma_start(x_plane[32 * q : 32 * q + 4, :].bitcast(I32), picked_bytes[P - 16 + 4 * q : P - 12 + 4 * q, :].bitcast(I32))
+            rows = slice(first_row + 4 * q, first_row + 4 * q + 4)
+            nc.sync.dma_start(x_plane[32 * q : 32 * q + 4, :].bitcast(I32), picked_bytes[rows, :].bitcast(I32))
         nc.sync.dma_start(w2_raw[1][:], w2_rows[:, :, H // 2 :])
-        w1_raw = keep.tile([P, PACK, N], F32, name="w1_raw")
-        nc.sync.dma_start(w1_raw[:], w1.rearrange("(p j) c -> p j c", j=PACK))
-        w3_raw = keep.tile([P, PACK, N], F32, name="w3_raw")
-        nc.sync.dma_start(w3_raw[:], w3.rearrange("(p j) c -> p j c", j=PACK))
+        w1_raw = keep.tile([P, SLOTS, N], F32, name="w1_raw")
+        nc.sync.dma_start(w1_raw[:], w1.rearrange("(p j) c -> p j c", j=SLOTS))
+        w3_raw = keep.tile([P, SLOTS, N], F32, name="w3_raw")
+        nc.sync.dma_start(w3_raw[:], w3.rearrange("(p j) c -> p j c", j=SLOTS))
 
         x_codes = []
         for g in range(S // GATHER):
-            codes = keep.tile([P, GATHER], U32, name=f"x_codes{g}", align_bytes=64)
-            cols = slice(g * GATHER // 16, (g + 1) * GATHER // 16)
-            nc.vector.tensor_copy(codes[:], word_table[:].bitcast(U32).indirect(offsets[:, cols]))
-            x_codes.append(codes)
+            picked_words = keep.tile([P, GATHER], U32, name=f"x_codes{g}", align_bytes=64)
+            entries = slice(g * GATHER // LIST_ROWS, (g + 1) * GATHER // LIST_ROWS)
+            nc.vector.tensor_copy(picked_words[:], word_table[:].bitcast(U32).indirect(offsets[:, entries]))
+            x_codes.append(picked_words)
 
         def bank_tile(bank, shape):
             return psum.tile([P] + shape, F32, name=f"bank{bank}")
 
         warm_bank = bank_tile(7, [GATHER])
-        for i in range(WARM):
+        for warm_pass in range(WARM_UP_PASSES):
             nc.tensor.matmul_mx(
                 warm_bank[:], x_codes[0][:, :P].bitcast(FP8X4), picked_bytes[:, :P],
                 x_codes[0][:].bitcast(FP8X4), picked_bytes[:, :GATHER], start=True, stop=True,
@@ -78,21 +81,21 @@ def tile_picked_lora_relu_p_kernel(tc, x_words, x_scales, w1, w2, w3, offs, out)
             g, lo = divmod(first, GATHER)
             return x_codes[g][:, lo : lo + count].bitcast(FP8X4), x_plane[:, first : first + count]
 
-        w2_grouped = [keep.tile([P, 2, P, PACK], BF16, name=f"w2_grouped{i}", align_bytes=64) for i in range(2)]
+        w2_grouped = [keep.tile([P, 2, P, SLOTS], BF16, name=f"w2_grouped{pair}", align_bytes=64) for pair in range(2)]
 
         def cast_w2(engine_copy, half, pair, lo, hi):
-            dst = w2_grouped[pair][:, :, half * 64 + lo : half * 64 + hi, :].rearrange("p t m j -> p m j t")
-            src = w2_raw[half][:, :, lo * PACK : hi * PACK].rearrange("p j (m t) -> p m j t", t=PACK)
+            dst = w2_grouped[pair][:, :, half * HALF + lo : half * HALF + hi, :].rearrange("p e m j -> p m j e")
+            src = w2_raw[half][:, :, lo * SLOTS : hi * SLOTS].rearrange("p j (m t) -> p m j t", t=SLOTS)
             engine_copy(dst, src[:, :, :, 2 * pair : 2 * pair + 2])
 
-        def cast_plain(engine_copy, grouped, raw, lo, hi):
+        def cast_columns(engine_copy, grouped, raw, lo, hi):
             engine_copy(
                 grouped[:, lo:hi, :].rearrange("p (c i) j -> p c j i", i=4),
                 raw[:, :, lo:hi].rearrange("p j (c i) -> p c j i", i=4),
             )
 
-        w3_grouped = keep.tile([P, N, PACK], BF16, name="w3_grouped", align_bytes=64)
-        w1_grouped = keep.tile([P, N, PACK], BF16, name="w1_grouped", align_bytes=64)
+        w3_grouped = keep.tile([P, N, SLOTS], BF16, name="w3_grouped", align_bytes=64)
+        w1_grouped = keep.tile([P, N, SLOTS], BF16, name="w1_grouped", align_bytes=64)
 
         def quantize(grouped, name):
             width = grouped.shape[1]
@@ -101,112 +104,116 @@ def tile_picked_lora_relu_p_kernel(tc, x_words, x_scales, w1, w2, w3, offs, out)
             nc.vector.quantize_mx(codes[:].bitcast(FP8X4), plane[:], grouped.rearrange("p c j -> p (c j)"))
             return codes, plane
 
-        cast_w2(nc.scalar.copy, 0, 0, 0, 64)
-        cast_w2(nc.scalar.copy, 0, 1, 0, 64)
-        cast_w2(nc.vector.tensor_copy, 1, 0, 0, 64)
-        cast_w2(nc.vector.tensor_copy, 1, 1, 0, W2_VECTOR_EXTRA)
-        cast_w2(nc.scalar.copy, 1, 1, W2_VECTOR_EXTRA, 64)
-        w2_q = [quantize(w2_grouped[i][:].rearrange("p t m j -> p (t m) j"), f"w2_{i}") for i in range(2)]
+        cast_w2(nc.scalar.copy, 0, 0, 0, HALF)
+        cast_w2(nc.scalar.copy, 0, 1, 0, HALF)
+        cast_w2(nc.vector.tensor_copy, 1, 0, 0, HALF)
+        cast_w2(nc.vector.tensor_copy, 1, 1, 0, W2_VECTOR_GROUPS)
+        cast_w2(nc.scalar.copy, 1, 1, W2_VECTOR_GROUPS, HALF)
+        w2_mx = [quantize(w2_grouped[pair][:].rearrange("p e m j -> p (e m) j"), f"w2_{pair}") for pair in range(2)]
 
-        h_grouped = keep.tile([P, S, PACK], BF16, name="h_grouped", align_bytes=64)
-        h_banks = [bank_tile(b, [PACK, BANK_TOKENS]) for b in range(S // BANK_TOKENS)]
+        h_grouped = keep.tile([P, S, SLOTS], BF16, name="h_grouped", align_bytes=64)
+        early_groups = S // GROUP - 2
+        h_banks = [bank_tile(group, [SLOTS, GROUP]) for group in range(early_groups)]
 
-        def hidden_pair(b, pair):
-            codes, plane = x_operand(b * BANK_TOKENS, BANK_TOKENS)
-            w2_codes, w2_plane = w2_q[pair]
+        def hidden_pair(group, pair):
+            x_mx = x_operand(group * GROUP, GROUP)
+            w2_codes, w2_plane = w2_mx[pair]
             for e in range(2):
                 cols = slice(e * P, (e + 1) * P)
                 nc.tensor.matmul_mx(
-                    h_banks[b][:, 2 * pair + e, :], w2_codes[:, cols].bitcast(FP8X4), w2_plane[:, cols],
-                    codes, plane, start=True, stop=True,
+                    h_banks[group][:, 2 * pair + e, :], w2_codes[:, cols].bitcast(FP8X4), w2_plane[:, cols],
+                    *x_mx, start=True, stop=True,
                 )
 
-        def relu_out(b, on_vector):
-            dst = h_grouped[:, b * BANK_TOKENS : (b + 1) * BANK_TOKENS, :]
-            src = h_banks[b][:].rearrange("p t n -> p n t")
-            if on_vector:
-                nc.vector.tensor_scalar_max(dst, src, 0.0)
-            else:
-                nc.scalar.activation(dst, src, RELU)
+        def late_hidden(group, bank):
+            h_banks.append(bank_tile(bank, [SLOTS, GROUP]))
+            for pair in range(2):
+                hidden_pair(group, pair)
 
-        def quantize_h(c):
-            first, count = CHUNKS[c]
-            return quantize(h_grouped[:, first : first + count, :], f"h{c}")
+        def h_views(group):
+            return h_grouped[:, group * GROUP : (group + 1) * GROUP, :], h_banks[group][:].rearrange("p t n -> p n t")
+
+        def relu_on_scalar(group):
+            nc.scalar.activation(*h_views(group), RELU)
+
+        def relu_on_vector(group):
+            nc.vector.tensor_scalar_max(*h_views(group), 0.0)
+
+        def quantize_h(chunk):
+            first, count = CHUNKS[chunk]
+            return quantize(h_grouped[:, first : first + count, :], f"h{chunk}")
 
         out_rows = out.rearrange("(u p) s -> p u s", p=P)
 
-        def own_pass(dst, c, u):
-            codes, plane = x_operand(*CHUNKS[c])
-            cols = slice(u * P, (u + 1) * P)
-            nc.tensor.matmul_mx(dst, w1_codes[:, cols].bitcast(FP8X4), w1_plane[:, cols], codes, plane, start=True, stop=False)
-
-        def adapter_pass(dst, u, h_q):
-            cols = slice(u * P, (u + 1) * P)
-            nc.tensor.matmul_mx(
-                dst, w3_codes[:, cols].bitcast(FP8X4), w3_plane[:, cols],
-                h_q[0][:].bitcast(FP8X4), h_q[1][:], start=False, stop=True,
-            )
-
-        def open_chunk(c, banks):
-            tiles = [bank_tile(bank, [CHUNKS[c][1]]) for bank in banks]
-            for u in range(N // P):
-                own_pass(tiles[u][:], c, u)
+        def open_chunk(chunk, banks):
+            tiles = [bank_tile(bank, [CHUNKS[chunk][1]]) for bank in banks]
+            for u, tile in enumerate(tiles):
+                cols = slice(u * P, (u + 1) * P)
+                nc.tensor.matmul_mx(
+                    tile[:], w1_codes[:, cols].bitcast(FP8X4), w1_plane[:, cols],
+                    *x_operand(*CHUNKS[chunk]), start=True, stop=False,
+                )
             return tiles
 
-        def close_chunk(tiles, h_q):
-            for u in range(N // P):
-                adapter_pass(tiles[u][:], u, h_q)
+        def close_chunk(tiles, h_mx):
+            h_codes, h_plane = h_mx
+            for u, tile in enumerate(tiles):
+                cols = slice(u * P, (u + 1) * P)
+                nc.tensor.matmul_mx(
+                    tile[:], w3_codes[:, cols].bitcast(FP8X4), w3_plane[:, cols],
+                    h_codes[:].bitcast(FP8X4), h_plane[:], start=False, stop=True,
+                )
 
-        def store_chunk(c, tiles, copies):
-            first, count = CHUNKS[c]
-            staged = keep.tile([P, N // P, count], F32, name=f"staged{c}")
-            for u in range(N // P):
-                copies[u](staged[:, u, :], tiles[u][:])
-                if count == 256:
-                    nc.sync.dma_start(out_rows[:, u, first : first + count], staged[:, u, :])
-            if count < 256:
-                nc.sync.dma_start(out_rows[:, :, first : first + count], staged[:])
+        def store_wide_chunk(chunk, tiles):
+            first, count = CHUNKS[chunk]
+            staged = keep.tile([P, N // P, count], F32, name=f"staged{chunk}")
+            for u, tile in enumerate(tiles):
+                nc.scalar.copy(staged[:, u, :], tile[:])
+                nc.sync.dma_start(out_rows[:, u, first : first + count], staged[:, u, :])
 
-        on_scalar = (nc.scalar.copy, nc.scalar.copy)
-        on_both = (nc.vector.tensor_copy, nc.scalar.copy)
+        def store_short_chunk(chunk, tiles):
+            first, count = CHUNKS[chunk]
+            staged = keep.tile([P, N // P, count], F32, name=f"staged{chunk}")
+            nc.vector.tensor_copy(staged[:, 0, :], tiles[0][:])
+            nc.scalar.copy(staged[:, 1, :], tiles[1][:])
+            nc.sync.dma_start(out_rows[:, :, first : first + count], staged[:])
 
         for pair in range(2):
-            for b in range(2):
-                hidden_pair(b, pair)
-        for b in range(2, 8):
+            for group in range(2):
+                hidden_pair(group, pair)
+        for group in range(2, early_groups):
             for pair in range(2):
-                hidden_pair(b, pair)
+                hidden_pair(group, pair)
 
-        cast_plain(nc.scalar.copy, w1_grouped, w1_raw, 0, W1_SCALAR)
-        cast_plain(nc.vector.tensor_copy, w1_grouped, w1_raw, W1_SCALAR, N)
-        relu_out(0, False)
-        relu_out(1, True)
-        relu_out(2, False)
+        cast_columns(nc.scalar.copy, w1_grouped, w1_raw, 0, W1_SCALAR_COLUMNS)
+        cast_columns(nc.vector.tensor_copy, w1_grouped, w1_raw, W1_SCALAR_COLUMNS, N)
+        relu_on_scalar(0)
+        relu_on_vector(1)
+        relu_on_scalar(2)
         w1_codes, w1_plane = quantize(w1_grouped[:], "w1")
-        cast_plain(nc.vector.tensor_copy, w3_grouped, w3_raw, 0, N)
-        relu_out(3, False)
-        h0 = quantize_h(0)
-        relu_out(4, False)
+        cast_columns(nc.vector.tensor_copy, w3_grouped, w3_raw, 0, N)
+        relu_on_scalar(3)
+        h_mx0 = quantize_h(0)
+        relu_on_scalar(4)
         w3_codes, w3_plane = quantize(w3_grouped[:], "w3")
+
         out0 = open_chunk(0, (0, 1))
-        close_chunk(out0, h0)
-        out1 = open_chunk(1, (2, 3))
-        relu_out(5, False)
-        h1 = quantize_h(1)
-        close_chunk(out1, h1)
-        store_chunk(0, out0, on_scalar)
-        out2 = open_chunk(2, (4, 5))
-        h2 = quantize_h(2)
-        close_chunk(out2, h2)
-        relu_out(6, True)
-        store_chunk(1, out1, on_scalar)
+        late_hidden(6, 3)
+        close_chunk(out0, h_mx0)
+        out1 = open_chunk(1, (2, 6))
+        late_hidden(7, 4)
+        relu_on_scalar(5)
+        close_chunk(out1, quantize_h(1))
+        store_wide_chunk(0, out0)
+        out2 = open_chunk(2, (7, 5))
+        close_chunk(out2, quantize_h(2))
+        relu_on_vector(6)
+        store_wide_chunk(1, out1)
         out3 = open_chunk(3, (0, 1))
-        relu_out(7, True)
-        h3 = quantize_h(3)
-        close_chunk(out3, h3)
-        out4 = open_chunk(4, (2, 3))
-        store_chunk(2, out2, on_scalar)
-        h4 = quantize_h(4)
-        close_chunk(out4, h4)
-        store_chunk(3, out3, on_both)
-        store_chunk(4, out4, on_both)
+        relu_on_vector(7)
+        close_chunk(out3, quantize_h(3))
+        out4 = open_chunk(4, (2, 6))
+        store_wide_chunk(2, out2)
+        close_chunk(out4, quantize_h(4))
+        store_short_chunk(3, out3)
+        store_short_chunk(4, out4)

@@ -51,11 +51,11 @@ def tile_picked_lora_relu_p_kernel(tc, x_words, x_scales, w1, w2, w3, offs, out)
         w2_rows = w2.rearrange("(p j) c -> p j c", j=SLOTS)
         w2_raw = [keep.tile([P, SLOTS, H // 2], F32, name=f"w2_raw{half}") for half in range(2)]
         nc.sync.dma_start(w2_raw[0][:], w2_rows[:, :, : H // 2])
+        nc.sync.dma_start(w2_raw[1][:], w2_rows[:, :, H // 2 :])
         for q in range(4):
             rows = slice(first_row + 4 * q, first_row + 4 * q + 4)
             nc.sync.dma_start(x_plane[32 * q : 32 * q + 4, :].bitcast(I32), picked_bytes[rows, :].bitcast(I32))
-        nc.sync.dma_start(w2_raw[1][:], w2_rows[:, :, H // 2 :])
-        w1_raw = keep.tile([P, SLOTS, N], F32, name="w1_raw")
+        w1_raw = keep.tile([P, SLOTS, N], F32, name="w1_then_h", align_bytes=64)
         nc.sync.dma_start(w1_raw[:], w1.rearrange("(p j) c -> p j c", j=SLOTS))
         w3_raw = keep.tile([P, SLOTS, N], F32, name="w3_raw")
         nc.sync.dma_start(w3_raw[:], w3.rearrange("(p j) c -> p j c", j=SLOTS))
@@ -111,7 +111,7 @@ def tile_picked_lora_relu_p_kernel(tc, x_words, x_scales, w1, w2, w3, offs, out)
         cast_w2(nc.scalar.copy, 1, 1, W2_VECTOR_GROUPS, HALF)
         w2_mx = [quantize(w2_grouped[pair][:].rearrange("p e m j -> p (e m) j"), f"w2_{pair}") for pair in range(2)]
 
-        h_grouped = keep.tile([P, S, SLOTS], BF16, name="h_grouped", align_bytes=64)
+        h_grouped = keep.tile([P, S, SLOTS], BF16, name="w1_then_h", align_bytes=64)
         early_groups = S // GROUP - 2
         h_banks = [bank_tile(group, [SLOTS, GROUP]) for group in range(early_groups)]
 

@@ -25,6 +25,7 @@ HALF = P // 2
 W2_VECTOR_GROUPS = 16
 W1_SCALAR_COLUMNS = 64
 WARM_UP_PASSES = 4
+X_HEAD = 3584
 
 
 def tile_picked_lora_relu_p_kernel(tc, x_words, x_scales, w1, w2, w3, offs, out):
@@ -43,50 +44,36 @@ def tile_picked_lora_relu_p_kernel(tc, x_words, x_scales, w1, w2, w3, offs, out)
         offsets = keep.tile([P, S // LIST_ROWS], U16, name="offsets")
         nc.sync.dma_start(offsets[:], offs)
         nc.sync.dma_start(scale_table[first_row:, :].bitcast(I32), x_scales[0].bitcast(I32))
-        nc.sync.dma_start(word_table[:], x_words[0].rearrange("p n t -> p (n t)").bitcast(I32))
+        w2_raw = keep.tile([P, SLOTS, H], F32, name="w2_raw")
+        nc.sync.dma_start(w2_raw[:], w2.rearrange("(p j) c -> p j c", j=SLOTS))
+        x_source = x_words[0].rearrange("p n t -> p (n t)").bitcast(I32)
+        nc.sync.dma_start(word_table[:, :X_HEAD], x_source[:, :X_HEAD])
 
         picked_bytes = keep.tile([P, S], U8, name="picked_bytes", align_bytes=64)
         nc.vector.tensor_copy(picked_bytes[:], scale_table[:].indirect(offsets[:]))
 
-        w2_rows = w2.rearrange("(p j) c -> p j c", j=SLOTS)
-        w2_raw = [keep.tile([P, SLOTS, H // 2], F32, name=f"w2_raw{half}") for half in range(2)]
-        nc.sync.dma_start(w2_raw[0][:], w2_rows[:, :, : H // 2])
-        nc.sync.dma_start(w2_raw[1][:], w2_rows[:, :, H // 2 :])
         for q in range(4):
             rows = slice(first_row + 4 * q, first_row + 4 * q + 4)
             nc.sync.dma_start(x_plane[32 * q : 32 * q + 4, :].bitcast(I32), picked_bytes[rows, :].bitcast(I32))
+        nc.sync.dma_start(word_table[:, X_HEAD:], x_source[:, X_HEAD:])
         w1_raw = keep.tile([P, SLOTS, N], F32, name="w1_then_h", align_bytes=64)
         nc.sync.dma_start(w1_raw[:], w1.rearrange("(p j) c -> p j c", j=SLOTS))
         w3_raw = keep.tile([P, SLOTS, N], F32, name="w3_raw")
         nc.sync.dma_start(w3_raw[:], w3.rearrange("(p j) c -> p j c", j=SLOTS))
 
-        x_codes = []
-        for g in range(S // GATHER):
-            picked_words = keep.tile([P, GATHER], U32, name=f"x_codes{g}", align_bytes=64)
-            entries = slice(g * GATHER // LIST_ROWS, (g + 1) * GATHER // LIST_ROWS)
-            nc.vector.tensor_copy(picked_words[:], word_table[:].bitcast(U32).indirect(offsets[:, entries]))
-            x_codes.append(picked_words)
-
         def bank_tile(bank, shape):
             return psum.tile([P] + shape, F32, name=f"bank{bank}")
-
-        warm_bank = bank_tile(7, [GATHER])
-        for warm_pass in range(WARM_UP_PASSES):
-            nc.tensor.matmul_mx(
-                warm_bank[:], x_codes[0][:, :P].bitcast(FP8X4), picked_bytes[:, :P],
-                x_codes[0][:].bitcast(FP8X4), picked_bytes[:, :GATHER], start=True, stop=True,
-            )
 
         def x_operand(first, count):
             g, lo = divmod(first, GATHER)
             return x_codes[g][:, lo : lo + count].bitcast(FP8X4), x_plane[:, first : first + count]
 
-        w2_grouped = [keep.tile([P, 2, P, SLOTS], BF16, name=f"w2_grouped{pair}", align_bytes=64) for pair in range(2)]
+        w2_grouped = keep.tile([P, SLOTS, P, SLOTS], BF16, name="w2_grouped", align_bytes=64)
 
-        def cast_w2(engine_copy, half, pair, lo, hi):
-            dst = w2_grouped[pair][:, :, half * HALF + lo : half * HALF + hi, :].rearrange("p e m j -> p m j e")
-            src = w2_raw[half][:, :, lo * SLOTS : hi * SLOTS].rearrange("p j (m t) -> p m j t", t=SLOTS)
-            engine_copy(dst, src[:, :, :, 2 * pair : 2 * pair + 2])
+        def cast_w2(engine_copy, lo, hi):
+            dst = w2_grouped[:, :, lo:hi, :].rearrange("p t m j -> p m j t")
+            src = w2_raw[:, :, lo * SLOTS : hi * SLOTS].rearrange("p j (m t) -> p m j t", t=SLOTS)
+            engine_copy(dst, src)
 
         def cast_columns(engine_copy, grouped, raw, lo, hi):
             engine_copy(
@@ -104,12 +91,23 @@ def tile_picked_lora_relu_p_kernel(tc, x_words, x_scales, w1, w2, w3, offs, out)
             nc.vector.quantize_mx(codes[:].bitcast(FP8X4), plane[:], grouped.rearrange("p c j -> p (c j)"))
             return codes, plane
 
-        cast_w2(nc.scalar.copy, 0, 0, 0, HALF)
-        cast_w2(nc.scalar.copy, 0, 1, 0, HALF)
-        cast_w2(nc.vector.tensor_copy, 1, 0, 0, HALF)
-        cast_w2(nc.vector.tensor_copy, 1, 1, 0, W2_VECTOR_GROUPS)
-        cast_w2(nc.scalar.copy, 1, 1, W2_VECTOR_GROUPS, HALF)
-        w2_mx = [quantize(w2_grouped[pair][:].rearrange("p e m j -> p (e m) j"), f"w2_{pair}") for pair in range(2)]
+        cast_w2(nc.scalar.copy, 0, HALF)
+        cast_w2(nc.vector.tensor_copy, HALF, P)
+        w2_codes, w2_plane = quantize(w2_grouped[:].rearrange("p t m j -> p (t m) j"), "w2")
+
+        warm_bank = bank_tile(7, [GATHER])
+        for warm_pass in range(WARM_UP_PASSES):
+            nc.tensor.matmul_mx(
+                warm_bank[:], w2_codes[:, :P].bitcast(FP8X4), w2_plane[:, :P],
+                w2_codes[:].bitcast(FP8X4), x_plane[:, :GATHER], start=True, stop=True,
+            )
+
+        x_codes = []
+        for g in range(S // GATHER):
+            picked_words = keep.tile([P, GATHER], U32, name=f"x_codes{g}", align_bytes=64)
+            entries = slice(g * GATHER // LIST_ROWS, (g + 1) * GATHER // LIST_ROWS)
+            nc.vector.tensor_copy(picked_words[:], word_table[:].bitcast(U32).indirect(offsets[:, entries]))
+            x_codes.append(picked_words)
 
         h_grouped = keep.tile([P, S, SLOTS], BF16, name="w1_then_h", align_bytes=64)
         early_groups = S // GROUP - 2
@@ -117,9 +115,8 @@ def tile_picked_lora_relu_p_kernel(tc, x_words, x_scales, w1, w2, w3, offs, out)
 
         def hidden_pair(group, pair):
             x_mx = x_operand(group * GROUP, GROUP)
-            w2_codes, w2_plane = w2_mx[pair]
             for e in range(2):
-                cols = slice(e * P, (e + 1) * P)
+                cols = slice((2 * pair + e) * P, (2 * pair + e + 1) * P)
                 nc.tensor.matmul_mx(
                     h_banks[group][:, 2 * pair + e, :], w2_codes[:, cols].bitcast(FP8X4), w2_plane[:, cols],
                     *x_mx, start=True, stop=True,
@@ -178,15 +175,11 @@ def tile_picked_lora_relu_p_kernel(tc, x_words, x_scales, w1, w2, w3, offs, out)
             nc.scalar.copy(staged[:, 1, :], tiles[1][:])
             nc.sync.dma_start(out_rows[:, :, first : first + count], staged[:])
 
-        for pair in range(2):
-            for group in range(2):
-                hidden_pair(group, pair)
-        for group in range(2, early_groups):
+        for group in range(early_groups):
             for pair in range(2):
                 hidden_pair(group, pair)
 
-        cast_columns(nc.scalar.copy, w1_grouped, w1_raw, 0, W1_SCALAR_COLUMNS)
-        cast_columns(nc.vector.tensor_copy, w1_grouped, w1_raw, W1_SCALAR_COLUMNS, N)
+        cast_columns(nc.scalar.copy, w1_grouped, w1_raw, 0, N)
         relu_on_scalar(0)
         relu_on_vector(1)
         relu_on_scalar(2)

@@ -26,6 +26,7 @@ W2_VECTOR_GROUPS = 16
 W1_SCALAR_COLUMNS = 64
 WARM_UP_PASSES = 4
 X_HEAD = 3584
+W2_SCALAR_GROUPS = 112
 
 
 def tile_picked_lora_relu_p_kernel(tc, x_words, x_scales, w1, w2, w3, offs, out):
@@ -91,15 +92,15 @@ def tile_picked_lora_relu_p_kernel(tc, x_words, x_scales, w1, w2, w3, offs, out)
             nc.vector.quantize_mx(codes[:].bitcast(FP8X4), plane[:], grouped.rearrange("p c j -> p (c j)"))
             return codes, plane
 
-        cast_w2(nc.scalar.copy, 0, HALF)
-        cast_w2(nc.vector.tensor_copy, HALF, P)
+        cast_w2(nc.scalar.copy, 0, W2_SCALAR_GROUPS)
+        cast_w2(nc.vector.tensor_copy, W2_SCALAR_GROUPS, P)
         w2_codes, w2_plane = quantize(w2_grouped[:].rearrange("p t m j -> p (t m) j"), "w2")
 
         warm_bank = bank_tile(7, [GATHER])
         for warm_pass in range(WARM_UP_PASSES):
             nc.tensor.matmul_mx(
                 warm_bank[:], w2_codes[:, :P].bitcast(FP8X4), w2_plane[:, :P],
-                w2_codes[:].bitcast(FP8X4), x_plane[:, :GATHER], start=True, stop=True,
+                w2_codes[:].bitcast(FP8X4), w2_plane[:], start=True, stop=True,
             )
 
         x_codes = []

@@ -24,7 +24,6 @@ CHUNKS = ((0, 256), (256, 256), (512, 256), (768, 128), (896, 128))
 HALF = P // 2
 W2_VECTOR_GROUPS = 16
 W1_SCALAR_COLUMNS = 64
-WARM_UP_PASSES = 4
 X_HEAD = 3584
 W2_SCALAR_GROUPS = 112
 
@@ -95,13 +94,6 @@ def tile_picked_lora_relu_p_kernel(tc, x_words, x_scales, w1, w2, w3, offs, out)
         cast_w2(nc.scalar.copy, 0, W2_SCALAR_GROUPS)
         cast_w2(nc.vector.tensor_copy, W2_SCALAR_GROUPS, P)
         w2_codes, w2_plane = quantize(w2_grouped[:].rearrange("p t m j -> p (t m) j"), "w2")
-
-        warm_bank = bank_tile(7, [GATHER])
-        for warm_pass in range(WARM_UP_PASSES):
-            nc.tensor.matmul_mx(
-                warm_bank[:], w2_codes[:, :P].bitcast(FP8X4), w2_plane[:, :P],
-                w2_codes[:].bitcast(FP8X4), w2_plane[:], start=True, stop=True,
-            )
 
         x_codes = []
         for g in range(S // GATHER):

@@ -24,6 +24,8 @@ CHUNKS = ((0, 256), (256, 256), (512, 256), (768, 128), (896, 128))
 HALF = P // 2
 W2_VECTOR_GROUPS = 16
 W1_SCALAR_COLUMNS = 64
+WARM_UP_PASSES = 4
+WARM_UP_ROWS = 32
 X_HEAD = 3584
 W2_SCALAR_GROUPS = 112
 
@@ -94,6 +96,13 @@ def tile_picked_lora_relu_p_kernel(tc, x_words, x_scales, w1, w2, w3, offs, out)
         cast_w2(nc.scalar.copy, 0, W2_SCALAR_GROUPS)
         cast_w2(nc.vector.tensor_copy, W2_SCALAR_GROUPS, P)
         w2_codes, w2_plane = quantize(w2_grouped[:].rearrange("p t m j -> p (t m) j"), "w2")
+
+        warm_bank = bank_tile(7, [GATHER])
+        for warm_pass in range(WARM_UP_PASSES):
+            nc.tensor.matmul_mx(
+                warm_bank[:WARM_UP_ROWS, :], w2_codes[:, :WARM_UP_ROWS].bitcast(FP8X4), w2_plane[:, :WARM_UP_ROWS],
+                w2_codes[:].bitcast(FP8X4), w2_plane[:], start=True, stop=True,
+            )
 
         x_codes = []
         for g in range(S // GATHER):

@@ -26,7 +26,6 @@ W2_VECTOR_GROUPS = 16
 W1_SCALAR_COLUMNS = 64
 WARM_UP_PASSES = 4
 WARM_UP_ROWS = 32
-X_HEAD = 3584
 W2_SCALAR_GROUPS = 112
 
 
@@ -36,30 +35,30 @@ def tile_picked_lora_relu_p_kernel(tc, x_words, x_scales, w1, w2, w3, offs, out)
         keep = ctx.enter_context(tc.tile_pool(name="keep", bufs=1))
         psum = ctx.enter_context(tc.psum_pool(name="psum", bufs=1))
 
-        first_row = P - BLOCKS
+        first_row, row_step = 32, 4
         scale_table = keep.tile([P, T], U8, name="scale_table", align_bytes=64)
-        nc.vector.memset(scale_table[:first_row, :].bitcast(I32), 0)
+        nc.vector.memset(scale_table[:].bitcast(I32), 0)
         x_plane = keep.tile([P, S], U8, name="x_plane", align_bytes=64)
         nc.gpsimd.memset(x_plane[:].bitcast(I32), 0)
 
         word_table = keep.tile([P, T], I32, name="word_table", align_bytes=64)
         offsets = keep.tile([P, S // LIST_ROWS], U16, name="offsets")
         nc.sync.dma_start(offsets[:], offs)
-        nc.sync.dma_start(scale_table[first_row:, :].bitcast(I32), x_scales[0].bitcast(I32))
         w2_raw = keep.tile([P, SLOTS, H], F32, name="w2_raw")
         nc.sync.dma_start(w2_raw[:], w2.rearrange("(p j) c -> p j c", j=SLOTS))
+        scale_rows = slice(first_row, first_row + BLOCKS * row_step, row_step)
+        nc.sync.dma_start(scale_table[scale_rows, :].bitcast(I32), x_scales[0].bitcast(I32))
         x_source = x_words[0].rearrange("p n t -> p (n t)").bitcast(I32)
-        nc.sync.dma_start(word_table[:, :X_HEAD], x_source[:, :X_HEAD])
+        nc.sync.dma_start(word_table[:], x_source)
 
         picked_bytes = keep.tile([P, S], U8, name="picked_bytes", align_bytes=64)
         nc.vector.tensor_copy(picked_bytes[:], scale_table[:].indirect(offsets[:]))
 
-        for q in range(4):
-            rows = slice(first_row + 4 * q, first_row + 4 * q + 4)
-            nc.sync.dma_start(x_plane[32 * q : 32 * q + 4, :].bitcast(I32), picked_bytes[rows, :].bitcast(I32))
-        nc.sync.dma_start(word_table[:, X_HEAD:], x_source[:, X_HEAD:])
         w1_raw = keep.tile([P, SLOTS, N], F32, name="w1_then_h", align_bytes=64)
         nc.sync.dma_start(w1_raw[:], w1.rearrange("(p j) c -> p j c", j=SLOTS))
+        for q in range(4):
+            rows = slice(first_row + 4 * q * row_step, first_row + (4 * q + 4) * row_step, row_step)
+            nc.sync.dma_start(x_plane[32 * q : 32 * q + 4, :].bitcast(I32), picked_bytes[rows, :].bitcast(I32))
         w3_raw = keep.tile([P, SLOTS, N], F32, name="w3_raw")
         nc.sync.dma_start(w3_raw[:], w3.rearrange("(p j) c -> p j c", j=SLOTS))
 
@@ -93,8 +92,7 @@ def tile_picked_lora_relu_p_kernel(tc, x_words, x_scales, w1, w2, w3, offs, out)
             nc.vector.quantize_mx(codes[:].bitcast(FP8X4), plane[:], grouped.rearrange("p c j -> p (c j)"))
             return codes, plane
 
-        cast_w2(nc.scalar.copy, 0, W2_SCALAR_GROUPS)
-        cast_w2(nc.vector.tensor_copy, W2_SCALAR_GROUPS, P)
+        cast_w2(nc.scalar.copy, 0, P)
         w2_codes, w2_plane = quantize(w2_grouped[:].rearrange("p t m j -> p (t m) j"), "w2")
 
         warm_bank = bank_tile(7, [GATHER])

@@ -18,15 +18,14 @@ P = 128
 SLOTS = 4
 BLOCKS = K // 32
 LIST_ROWS = 16
+QUADRANT = 32
+QUADRANT_ROWS = 4
+TABLE_FIRST, TABLE_STEP = 32, 4
 GATHER = 512
 GROUP = 128
 CHUNKS = ((0, 256), (256, 256), (512, 256), (768, 128), (896, 128))
-HALF = P // 2
-W2_VECTOR_GROUPS = 16
-W1_SCALAR_COLUMNS = 64
 WARM_UP_PASSES = 4
 WARM_UP_ROWS = 32
-W2_SCALAR_GROUPS = 112
 
 
 def tile_picked_lora_relu_p_kernel(tc, x_words, x_scales, w1, w2, w3, offs, out):
@@ -35,7 +34,9 @@ def tile_picked_lora_relu_p_kernel(tc, x_words, x_scales, w1, w2, w3, offs, out)
         keep = ctx.enter_context(tc.tile_pool(name="keep", bufs=1))
         psum = ctx.enter_context(tc.psum_pool(name="psum", bufs=1))
 
-        first_row, row_step = 32, 4
+        def table_rows(first, count):
+            return slice(TABLE_FIRST + first * TABLE_STEP, TABLE_FIRST + (first + count) * TABLE_STEP, TABLE_STEP)
+
         scale_table = keep.tile([P, T], U8, name="scale_table", align_bytes=64)
         nc.vector.memset(scale_table[:].bitcast(I32), 0)
         x_plane = keep.tile([P, S], U8, name="x_plane", align_bytes=64)
@@ -43,22 +44,22 @@ def tile_picked_lora_relu_p_kernel(tc, x_words, x_scales, w1, w2, w3, offs, out)
 
         word_table = keep.tile([P, T], I32, name="word_table", align_bytes=64)
         offsets = keep.tile([P, S // LIST_ROWS], U16, name="offsets")
-        nc.sync.dma_start(offsets[:], offs)
         w2_raw = keep.tile([P, SLOTS, H], F32, name="w2_raw")
         nc.sync.dma_start(w2_raw[:], w2.rearrange("(p j) c -> p j c", j=SLOTS))
-        scale_rows = slice(first_row, first_row + BLOCKS * row_step, row_step)
-        nc.sync.dma_start(scale_table[scale_rows, :].bitcast(I32), x_scales[0].bitcast(I32))
-        x_source = x_words[0].rearrange("p n t -> p (n t)").bitcast(I32)
-        nc.sync.dma_start(word_table[:], x_source)
+        nc.sync.dma_start(offsets[:], offs)
+        nc.sync.dma_start(scale_table[table_rows(0, BLOCKS), :].bitcast(I32), x_scales[0].bitcast(I32))
+        nc.sync.dma_start(word_table[:], x_words[0].rearrange("p n t -> p (n t)").bitcast(I32))
 
         picked_bytes = keep.tile([P, S], U8, name="picked_bytes", align_bytes=64)
         nc.vector.tensor_copy(picked_bytes[:], scale_table[:].indirect(offsets[:]))
 
         w1_raw = keep.tile([P, SLOTS, N], F32, name="w1_then_h", align_bytes=64)
         nc.sync.dma_start(w1_raw[:], w1.rearrange("(p j) c -> p j c", j=SLOTS))
-        for q in range(4):
-            rows = slice(first_row + 4 * q * row_step, first_row + (4 * q + 4) * row_step, row_step)
-            nc.sync.dma_start(x_plane[32 * q : 32 * q + 4, :].bitcast(I32), picked_bytes[rows, :].bitcast(I32))
+        for q in range(P // QUADRANT):
+            nc.sync.dma_start(
+                x_plane[QUADRANT * q : QUADRANT * q + QUADRANT_ROWS, :].bitcast(I32),
+                picked_bytes[table_rows(QUADRANT_ROWS * q, QUADRANT_ROWS), :].bitcast(I32),
+            )
         w3_raw = keep.tile([P, SLOTS, N], F32, name="w3_raw")
         nc.sync.dma_start(w3_raw[:], w3.rearrange("(p j) c -> p j c", j=SLOTS))
 
@@ -71,15 +72,10 @@ def tile_picked_lora_relu_p_kernel(tc, x_words, x_scales, w1, w2, w3, offs, out)
 
         w2_grouped = keep.tile([P, SLOTS, P, SLOTS], BF16, name="w2_grouped", align_bytes=64)
 
-        def cast_w2(engine_copy, lo, hi):
-            dst = w2_grouped[:, :, lo:hi, :].rearrange("p t m j -> p m j t")
-            src = w2_raw[:, :, lo * SLOTS : hi * SLOTS].rearrange("p j (m t) -> p m j t", t=SLOTS)
-            engine_copy(dst, src)
-
-        def cast_columns(engine_copy, grouped, raw, lo, hi):
+        def cast_columns(engine_copy, grouped, raw):
             engine_copy(
-                grouped[:, lo:hi, :].rearrange("p (c i) j -> p c j i", i=4),
-                raw[:, :, lo:hi].rearrange("p j (c i) -> p c j i", i=4),
+                grouped[:].rearrange("p (c i) j -> p c j i", i=4),
+                raw[:].rearrange("p j (c i) -> p c j i", i=4),
             )
 
         w3_grouped = keep.tile([P, N, SLOTS], BF16, name="w3_grouped", align_bytes=64)
@@ -92,10 +88,13 @@ def tile_picked_lora_relu_p_kernel(tc, x_words, x_scales, w1, w2, w3, offs, out)
             nc.vector.quantize_mx(codes[:].bitcast(FP8X4), plane[:], grouped.rearrange("p c j -> p (c j)"))
             return codes, plane
 
-        cast_w2(nc.scalar.copy, 0, P)
+        nc.scalar.copy(
+            w2_grouped[:].rearrange("p t m j -> p m j t"),
+            w2_raw[:].rearrange("p j (m t) -> p m j t", t=SLOTS),
+        )
         w2_codes, w2_plane = quantize(w2_grouped[:].rearrange("p t m j -> p (t m) j"), "w2")
 
-        warm_bank = bank_tile(7, [GATHER])
+        warm_bank = bank_tile(7, [H])
         for warm_pass in range(WARM_UP_PASSES):
             nc.tensor.matmul_mx(
                 warm_bank[:WARM_UP_ROWS, :], w2_codes[:, :WARM_UP_ROWS].bitcast(FP8X4), w2_plane[:, :WARM_UP_ROWS],
@@ -113,19 +112,18 @@ def tile_picked_lora_relu_p_kernel(tc, x_words, x_scales, w1, w2, w3, offs, out)
         early_groups = S // GROUP - 2
         h_banks = [bank_tile(group, [SLOTS, GROUP]) for group in range(early_groups)]
 
-        def hidden_pair(group, pair):
+        def hidden(group):
             x_mx = x_operand(group * GROUP, GROUP)
-            for e in range(2):
-                cols = slice((2 * pair + e) * P, (2 * pair + e + 1) * P)
+            for t in range(SLOTS):
+                cols = slice(t * P, (t + 1) * P)
                 nc.tensor.matmul_mx(
-                    h_banks[group][:, 2 * pair + e, :], w2_codes[:, cols].bitcast(FP8X4), w2_plane[:, cols],
+                    h_banks[group][:, t, :], w2_codes[:, cols].bitcast(FP8X4), w2_plane[:, cols],
                     *x_mx, start=True, stop=True,
                 )
 
         def late_hidden(group, bank):
             h_banks.append(bank_tile(bank, [SLOTS, GROUP]))
-            for pair in range(2):
-                hidden_pair(group, pair)
+            hidden(group)
 
         def h_views(group):
             return h_grouped[:, group * GROUP : (group + 1) * GROUP, :], h_banks[group][:].rearrange("p t n -> p n t")
@@ -176,15 +174,14 @@ def tile_picked_lora_relu_p_kernel(tc, x_words, x_scales, w1, w2, w3, offs, out)
             nc.sync.dma_start(out_rows[:, :, first : first + count], staged[:])
 
         for group in range(early_groups):
-            for pair in range(2):
-                hidden_pair(group, pair)
+            hidden(group)
 
-        cast_columns(nc.scalar.copy, w1_grouped, w1_raw, 0, N)
+        cast_columns(nc.scalar.copy, w1_grouped, w1_raw)
         relu_on_scalar(0)
         relu_on_vector(1)
         relu_on_scalar(2)
         w1_codes, w1_plane = quantize(w1_grouped[:], "w1")
-        cast_columns(nc.vector.tensor_copy, w3_grouped, w3_raw, 0, N)
+        cast_columns(nc.vector.tensor_copy, w3_grouped, w3_raw)
         relu_on_scalar(3)
         h_mx0 = quantize_h(0)
         relu_on_scalar(4)

@@ -159,19 +159,24 @@ def tile_picked_lora_relu_p_kernel(tc, x_words, x_scales, w1, w2, w3, offs, out)
                     h_codes[:].bitcast(FP8X4), h_plane[:], start=False, stop=True,
                 )
 
-        def store_wide_chunk(chunk, tiles):
-            first, count = CHUNKS[chunk]
-            staged = keep.tile([P, N // P, count], F32, name=f"staged{chunk}")
-            for u, tile in enumerate(tiles):
-                nc.scalar.copy(staged[:, u, :], tile[:])
-                nc.sync.dma_start(out_rows[:, u, first : first + count], staged[:, u, :])
+        staged = [keep.tile([P, S], F32, name=f"staged{u}") for u in range(N // P)]
 
-        def store_short_chunk(chunk, tiles):
+        def empty(engine_copy, chunk, tiles, u):
             first, count = CHUNKS[chunk]
-            staged = keep.tile([P, N // P, count], F32, name=f"staged{chunk}")
-            nc.vector.tensor_copy(staged[:, 0, :], tiles[0][:])
-            nc.scalar.copy(staged[:, 1, :], tiles[1][:])
-            nc.sync.dma_start(out_rows[:, :, first : first + count], staged[:])
+            engine_copy(staged[u][:, first : first + count], tiles[u][:])
+
+        def store(u, first_chunk, last_chunk):
+            tokens = slice(CHUNKS[first_chunk][0], sum(CHUNKS[last_chunk]))
+            nc.sync.dma_start(out_rows[:, u, tokens], staged[u][:, tokens])
+
+        def store_wide_chunk(chunk, tiles):
+            for u in range(N // P):
+                empty(nc.scalar.copy, chunk, tiles, u)
+                store(u, chunk, chunk)
+
+        def empty_short_chunk(chunk, tiles):
+            empty(nc.vector.tensor_copy, chunk, tiles, 0)
+            empty(nc.scalar.copy, chunk, tiles, 1)
 
         for group in range(early_groups):
             hidden(group)
@@ -203,7 +208,12 @@ def tile_picked_lora_relu_p_kernel(tc, x_words, x_scales, w1, w2, w3, offs, out)
         relu_on_vector(7)
         close_chunk(out3, quantize_h(3))
         out4 = open_chunk(4, (2, 6))
-        store_wide_chunk(2, out2)
+        empty(nc.scalar.copy, 2, out2, 0)
+        store(0, 2, 2)
+        empty(nc.scalar.copy, 2, out2, 1)
         close_chunk(out4, quantize_h(4))
-        store_short_chunk(3, out3)
-        store_short_chunk(4, out4)
+        empty_short_chunk(3, out3)
+        store(1, 2, 3)
+        empty_short_chunk(4, out4)
+        store(0, 3, 4)
+        store(1, 4, 4)

@@ -74,8 +74,8 @@ def tile_picked_lora_relu_p_kernel(tc, x_words, x_scales, w1, w2, w3, offs, out)
 
         def cast_columns(engine_copy, grouped, raw):
             engine_copy(
-                grouped[:].rearrange("p (c i) j -> p c j i", i=4),
-                raw[:].rearrange("p j (c i) -> p c j i", i=4),
+                grouped[:].rearrange("p (c i) j -> p c j i", i=2),
+                raw[:].rearrange("p j (c i) -> p c j i", i=2),
             )
 
         w3_grouped = keep.tile([P, N, SLOTS], BF16, name="w3_grouped", align_bytes=64)

@@ -53,8 +53,10 @@ def tile_picked_lora_relu_p_kernel(tc, x_words, x_scales, w1, w2, w3, offs, out)
         picked_bytes = keep.tile([P, S], U8, name="picked_bytes", align_bytes=64)
         nc.vector.tensor_copy(picked_bytes[:], scale_table[:].indirect(offsets[:]))
 
-        w1_raw = keep.tile([P, SLOTS, N], F32, name="w1_then_h", align_bytes=64)
-        nc.sync.dma_start(w1_raw[:], w1.rearrange("(p j) c -> p j c", j=SLOTS))
+        w1_rows = w1.rearrange("(p j) c -> p j c", j=SLOTS)
+        w1_raw = [keep.tile([P, 2, N], F32, name=name, align_bytes=64) for name in ("w1_first_pair", "w1_then_h")]
+        for pair, raw in enumerate(w1_raw):
+            nc.sync.dma_start(raw[:], w1_rows[:, 2 * pair : 2 * pair + 2, :])
         for q in range(P // QUADRANT):
             nc.sync.dma_start(
                 x_plane[QUADRANT * q : QUADRANT * q + QUADRANT_ROWS, :].bitcast(I32),
@@ -74,7 +76,7 @@ def tile_picked_lora_relu_p_kernel(tc, x_words, x_scales, w1, w2, w3, offs, out)
 
         def cast_columns(engine_copy, grouped, raw):
             engine_copy(
-                grouped[:].rearrange("p (c i) j -> p c j i", i=2),
+                grouped.rearrange("p (c i) j -> p c j i", i=2),
                 raw[:].rearrange("p j (c i) -> p c j i", i=2),
             )
 
@@ -153,9 +155,9 @@ def tile_picked_lora_relu_p_kernel(tc, x_words, x_scales, w1, w2, w3, offs, out)
         def close_chunk(tiles, h_mx):
             h_codes, h_plane = h_mx
             for u, tile in enumerate(tiles):
-                cols = slice(u * P, (u + 1) * P)
+                w3_codes, w3_plane = w3_mx[u]
                 nc.tensor.matmul_mx(
-                    tile[:], w3_codes[:, cols].bitcast(FP8X4), w3_plane[:, cols],
+                    tile[:], w3_codes[:].bitcast(FP8X4), w3_plane[:],
                     h_codes[:].bitcast(FP8X4), h_plane[:], start=False, stop=True,
                 )
 
@@ -181,16 +183,17 @@ def tile_picked_lora_relu_p_kernel(tc, x_words, x_scales, w1, w2, w3, offs, out)
         for group in range(early_groups):
             hidden(group)
 
-        cast_columns(nc.scalar.copy, w1_grouped, w1_raw)
+        for pair, raw in enumerate(w1_raw):
+            cast_columns(nc.scalar.copy, w1_grouped[:, :, 2 * pair : 2 * pair + 2], raw)
         relu_on_scalar(0)
         relu_on_vector(1)
         relu_on_scalar(2)
         w1_codes, w1_plane = quantize(w1_grouped[:], "w1")
-        cast_columns(nc.vector.tensor_copy, w3_grouped, w3_raw)
+        cast_columns(nc.vector.tensor_copy, w3_grouped[:], w3_raw)
         relu_on_scalar(3)
         h_mx0 = quantize_h(0)
         relu_on_scalar(4)
-        w3_codes, w3_plane = quantize(w3_grouped[:], "w3")
+        w3_mx = [quantize(w3_grouped[:, u * P : (u + 1) * P, :], f"w3_{u}") for u in range(N // P)]
 
         out0 = open_chunk(0, (0, 1))
         late_hidden(6, 3)

@@ -21,7 +21,8 @@ LIST_ROWS = 16
 QUADRANT = 32
 QUADRANT_ROWS = 4
 TABLE_FIRST, TABLE_STEP = 32, 4
-GATHER = 512
+GATHERS = ((0, 256), (256, 256), (512, 512))
+W1_BY_PAIRS = 176
 GROUP = 128
 CHUNKS = ((0, 256), (256, 256), (512, 256), (768, 128), (896, 128))
 WARM_UP_PASSES = 4
@@ -54,9 +55,9 @@ def tile_picked_lora_relu_p_kernel(tc, x_words, x_scales, w1, w2, w3, offs, out)
         nc.vector.tensor_copy(picked_bytes[:], scale_table[:].indirect(offsets[:]))
 
         w1_rows = w1.rearrange("(p j) c -> p j c", j=SLOTS)
-        w1_raw = [keep.tile([P, 2, N], F32, name=name, align_bytes=64) for name in ("w1_first_pair", "w1_then_h")]
-        for pair, raw in enumerate(w1_raw):
-            nc.sync.dma_start(raw[:], w1_rows[:, 2 * pair : 2 * pair + 2, :])
+        w1_raw = keep.tile([P, SLOTS, N], F32, name="w1_then_h", align_bytes=64)
+        for pair in (slice(0, 2), slice(2, 4)):
+            nc.sync.dma_start(w1_raw[:, pair, :], w1_rows[:, pair, :])
         for q in range(P // QUADRANT):
             nc.sync.dma_start(
                 x_plane[QUADRANT * q : QUADRANT * q + QUADRANT_ROWS, :].bitcast(I32),
@@ -69,7 +70,8 @@ def tile_picked_lora_relu_p_kernel(tc, x_words, x_scales, w1, w2, w3, offs, out)
             return psum.tile([P] + shape, F32, name=f"bank{bank}")
 
         def x_operand(first, count):
-            g, lo = divmod(first, GATHER)
+            g = max(i for i, (start, size) in enumerate(GATHERS) if start <= first)
+            lo = first - GATHERS[g][0]
             return x_codes[g][:, lo : lo + count].bitcast(FP8X4), x_plane[:, first : first + count]
 
         w2_grouped = keep.tile([P, SLOTS, P, SLOTS], BF16, name="w2_grouped", align_bytes=64)
@@ -77,7 +79,7 @@ def tile_picked_lora_relu_p_kernel(tc, x_words, x_scales, w1, w2, w3, offs, out)
         def cast_columns(engine_copy, grouped, raw):
             engine_copy(
                 grouped.rearrange("p (c i) j -> p c j i", i=2),
-                raw[:].rearrange("p j (c i) -> p c j i", i=2),
+                raw.rearrange("p j (c i) -> p c j i", i=2),
             )
 
         w3_grouped = keep.tile([P, N, SLOTS], BF16, name="w3_grouped", align_bytes=64)
@@ -104,9 +106,9 @@ def tile_picked_lora_relu_p_kernel(tc, x_words, x_scales, w1, w2, w3, offs, out)
             )
 
         x_codes = []
-        for g in range(S // GATHER):
-            picked_words = keep.tile([P, GATHER], U32, name=f"x_codes{g}", align_bytes=64)
-            entries = slice(g * GATHER // LIST_ROWS, (g + 1) * GATHER // LIST_ROWS)
+        for g, (first, count) in enumerate(GATHERS):
+            picked_words = keep.tile([P, count], U32, name=f"x_codes{g}", align_bytes=64)
+            entries = slice(first // LIST_ROWS, (first + count) // LIST_ROWS)
             nc.vector.tensor_copy(picked_words[:], word_table[:].bitcast(U32).indirect(offsets[:, entries]))
             x_codes.append(picked_words)
 
@@ -183,13 +185,14 @@ def tile_picked_lora_relu_p_kernel(tc, x_words, x_scales, w1, w2, w3, offs, out)
         for group in range(early_groups):
             hidden(group)
 
-        for pair, raw in enumerate(w1_raw):
-            cast_columns(nc.scalar.copy, w1_grouped[:, :, 2 * pair : 2 * pair + 2], raw)
+        for pair in (slice(0, 2), slice(2, 4)):
+            cast_columns(nc.scalar.copy, w1_grouped[:, :W1_BY_PAIRS, pair], w1_raw[:, pair, :W1_BY_PAIRS])
+        cast_columns(nc.scalar.copy, w1_grouped[:, W1_BY_PAIRS:, :], w1_raw[:, :, W1_BY_PAIRS:])
         relu_on_scalar(0)
+        w1_codes, w1_plane = quantize(w1_grouped[:], "w1")
         relu_on_vector(1)
         relu_on_scalar(2)
-        w1_codes, w1_plane = quantize(w1_grouped[:], "w1")
-        cast_columns(nc.vector.tensor_copy, w3_grouped[:], w3_raw)
+        cast_columns(nc.vector.tensor_copy, w3_grouped[:], w3_raw[:])
         relu_on_scalar(3)
         h_mx0 = quantize_h(0)
         relu_on_scalar(4)
@@ -211,12 +214,9 @@ def tile_picked_lora_relu_p_kernel(tc, x_words, x_scales, w1, w2, w3, offs, out)
         relu_on_vector(7)
         close_chunk(out3, quantize_h(3))
         out4 = open_chunk(4, (2, 6))
-        empty(nc.scalar.copy, 2, out2, 0)
-        store(0, 2, 2)
-        empty(nc.scalar.copy, 2, out2, 1)
+        store_wide_chunk(2, out2)
         close_chunk(out4, quantize_h(4))
         empty_short_chunk(3, out3)
-        store(1, 2, 3)
         empty_short_chunk(4, out4)
-        store(0, 3, 4)
-        store(1, 4, 4)
+        for u in range(N // P):
+            store(u, 3, 4)

@@ -15,6 +15,7 @@ FP8X4 = mybir.dt.float8_e4m3fn_x4
 RELU = mybir.ActivationFunctionType.Relu
 
 P = 128
+DMA_BURST = 256
 SLOTS = 4
 BLOCKS = K // 32
 LIST_ROWS = 16
@@ -38,24 +39,24 @@ def tile_picked_lora_relu_p_kernel(tc, x_words, x_scales, w1, w2, w3, offs, out)
         def table_rows(first, count):
             return slice(TABLE_FIRST + first * TABLE_STEP, TABLE_FIRST + (first + count) * TABLE_STEP, TABLE_STEP)
 
-        scale_table = keep.tile([P, T], U8, name="scale_table", align_bytes=64)
+        scale_table = keep.tile([P, T], U8, name="scale_table", align_bytes=DMA_BURST)
         nc.vector.memset(scale_table[:].bitcast(I32), 0)
-        x_plane = keep.tile([P, S], U8, name="x_plane", align_bytes=64)
+        x_plane = keep.tile([P, S], U8, name="x_plane", align_bytes=DMA_BURST)
         nc.gpsimd.memset(x_plane[:].bitcast(I32), 0)
 
-        word_table = keep.tile([P, T], I32, name="word_table", align_bytes=64)
-        offsets = keep.tile([P, S // LIST_ROWS], U16, name="offsets")
-        w2_raw = keep.tile([P, SLOTS, H], F32, name="w2_raw")
+        word_table = keep.tile([P, T], I32, name="word_table", align_bytes=DMA_BURST)
+        offsets = keep.tile([P, S // LIST_ROWS], U16, name="offsets", align_bytes=DMA_BURST)
+        w2_raw = keep.tile([P, SLOTS, H], F32, name="w2_raw", align_bytes=DMA_BURST)
         nc.sync.dma_start(w2_raw[:], w2.rearrange("(p j) c -> p j c", j=SLOTS))
         nc.sync.dma_start(offsets[:], offs)
         nc.sync.dma_start(scale_table[table_rows(0, BLOCKS), :].bitcast(I32), x_scales[0].bitcast(I32))
         nc.sync.dma_start(word_table[:], x_words[0].rearrange("p n t -> p (n t)").bitcast(I32))
 
-        picked_bytes = keep.tile([P, S], U8, name="picked_bytes", align_bytes=64)
+        picked_bytes = keep.tile([P, S], U8, name="picked_bytes", align_bytes=DMA_BURST)
         nc.vector.tensor_copy(picked_bytes[:], scale_table[:].indirect(offsets[:]))
 
         w1_rows = w1.rearrange("(p j) c -> p j c", j=SLOTS)
-        w1_raw = keep.tile([P, SLOTS, N], F32, name="w1_then_h", align_bytes=64)
+        w1_raw = keep.tile([P, SLOTS, N], F32, name="w1_then_h", align_bytes=DMA_BURST)
         for pair in (slice(0, 2), slice(2, 4)):
             nc.sync.dma_start(w1_raw[:, pair, :], w1_rows[:, pair, :])
         for q in range(P // QUADRANT):
@@ -63,7 +64,7 @@ def tile_picked_lora_relu_p_kernel(tc, x_words, x_scales, w1, w2, w3, offs, out)
                 x_plane[QUADRANT * q : QUADRANT * q + QUADRANT_ROWS, :].bitcast(I32),
                 picked_bytes[table_rows(QUADRANT_ROWS * q, QUADRANT_ROWS), :].bitcast(I32),
             )
-        w3_raw = keep.tile([P, SLOTS, N], F32, name="w3_raw")
+        w3_raw = keep.tile([P, SLOTS, N], F32, name="w3_raw", align_bytes=DMA_BURST)
         nc.sync.dma_start(w3_raw[:], w3.rearrange("(p j) c -> p j c", j=SLOTS))
 
         def bank_tile(bank, shape):
@@ -112,7 +113,7 @@ def tile_picked_lora_relu_p_kernel(tc, x_words, x_scales, w1, w2, w3, offs, out)
             nc.vector.tensor_copy(picked_words[:], word_table[:].bitcast(U32).indirect(offsets[:, entries]))
             x_codes.append(picked_words)
 
-        h_grouped = keep.tile([P, S, SLOTS], BF16, name="w1_then_h", align_bytes=64)
+        h_grouped = keep.tile([P, S, SLOTS], BF16, name="w1_then_h", align_bytes=DMA_BURST)
         early_groups = S // GROUP - 2
         h_banks = [bank_tile(group, [SLOTS, GROUP]) for group in range(early_groups)]
 
@@ -163,7 +164,7 @@ def tile_picked_lora_relu_p_kernel(tc, x_words, x_scales, w1, w2, w3, offs, out)
                     h_codes[:].bitcast(FP8X4), h_plane[:], start=False, stop=True,
                 )
 
-        staged = [keep.tile([P, S], F32, name=f"staged{u}") for u in range(N // P)]
+        staged = [keep.tile([P, S], F32, name=f"staged{u}", align_bytes=DMA_BURST) for u in range(N // P)]
 
         def empty(engine_copy, chunk, tiles, u):
             first, count = CHUNKS[chunk]

@@ -164,24 +164,23 @@ def tile_picked_lora_relu_p_kernel(tc, x_words, x_scales, w1, w2, w3, offs, out)
                     h_codes[:].bitcast(FP8X4), h_plane[:], start=False, stop=True,
                 )
 
-        staged = [keep.tile([P, S], F32, name=f"staged{u}", align_bytes=DMA_BURST) for u in range(N // P)]
+        staged = keep.tile([P, N // P, S], F32, name="staged", align_bytes=DMA_BURST)
 
         def empty(engine_copy, chunk, tiles, u):
             first, count = CHUNKS[chunk]
-            engine_copy(staged[u][:, first : first + count], tiles[u][:])
-
-        def store(u, first_chunk, last_chunk):
-            tokens = slice(CHUNKS[first_chunk][0], sum(CHUNKS[last_chunk]))
-            nc.sync.dma_start(out_rows[:, u, tokens], staged[u][:, tokens])
+            engine_copy(staged[:, u, first : first + count], tiles[u][:])
 
         def store_wide_chunk(chunk, tiles):
+            first, count = CHUNKS[chunk]
             for u in range(N // P):
                 empty(nc.scalar.copy, chunk, tiles, u)
-                store(u, chunk, chunk)
+                nc.sync.dma_start(out_rows[:, u, first : first + count], staged[:, u, first : first + count])
 
-        def empty_short_chunk(chunk, tiles):
+        def store_short_chunk(chunk, tiles):
+            first, count = CHUNKS[chunk]
             empty(nc.vector.tensor_copy, chunk, tiles, 0)
             empty(nc.scalar.copy, chunk, tiles, 1)
+            nc.sync.dma_start(out_rows[:, :, first : first + count], staged[:, :, first : first + count])
 
         for group in range(early_groups):
             hidden(group)
@@ -217,7 +216,5 @@ def tile_picked_lora_relu_p_kernel(tc, x_words, x_scales, w1, w2, w3, offs, out)
         out4 = open_chunk(4, (2, 6))
         store_wide_chunk(2, out2)
         close_chunk(out4, quantize_h(4))
-        empty_short_chunk(3, out3)
-        empty_short_chunk(4, out4)
-        for u in range(N // P):
-            store(u, 3, 4)
+        store_short_chunk(3, out3)
+        store_short_chunk(4, out4)

@@ -23,7 +23,6 @@ QUADRANT = 32
 QUADRANT_ROWS = 4
 TABLE_FIRST, TABLE_STEP = 32, 4
 GATHERS = ((0, 256), (256, 256), (512, 512))
-W1_BY_PAIRS = 176
 GROUP = 128
 CHUNKS = ((0, 256), (256, 256), (512, 256), (768, 128), (896, 128))
 WARM_UP_PASSES = 4
@@ -55,15 +54,15 @@ def tile_picked_lora_relu_p_kernel(tc, x_words, x_scales, w1, w2, w3, offs, out)
         picked_bytes = keep.tile([P, S], U8, name="picked_bytes", align_bytes=DMA_BURST)
         nc.vector.tensor_copy(picked_bytes[:], scale_table[:].indirect(offsets[:]))
 
-        w1_rows = w1.rearrange("(p j) c -> p j c", j=SLOTS)
-        w1_raw = keep.tile([P, SLOTS, N], F32, name="w1_then_h", align_bytes=DMA_BURST)
-        for pair in (slice(0, 2), slice(2, 4)):
-            nc.sync.dma_start(w1_raw[:, pair, :], w1_rows[:, pair, :])
+        w1_rows = w1.rearrange("(p j) (u c) -> p u j c", j=SLOTS, c=P)
+        w1_raw = keep.tile([P, N // P, SLOTS, P], F32, name="w1_then_h", align_bytes=DMA_BURST)
+        nc.sync.dma_start(w1_raw[:, 0], w1_rows[:, 0])
         for q in range(P // QUADRANT):
             nc.sync.dma_start(
                 x_plane[QUADRANT * q : QUADRANT * q + QUADRANT_ROWS, :].bitcast(I32),
                 picked_bytes[table_rows(QUADRANT_ROWS * q, QUADRANT_ROWS), :].bitcast(I32),
             )
+        nc.sync.dma_start(w1_raw[:, 1], w1_rows[:, 1])
         w3_raw = keep.tile([P, SLOTS, N], F32, name="w3_raw", align_bytes=DMA_BURST)
         nc.sync.dma_start(w3_raw[:], w3.rearrange("(p j) c -> p j c", j=SLOTS))
 
@@ -185,9 +184,8 @@ def tile_picked_lora_relu_p_kernel(tc, x_words, x_scales, w1, w2, w3, offs, out)
         for group in range(early_groups):
             hidden(group)
 
-        for pair in (slice(0, 2), slice(2, 4)):
-            cast_columns(nc.scalar.copy, w1_grouped[:, :W1_BY_PAIRS, pair], w1_raw[:, pair, :W1_BY_PAIRS])
-        cast_columns(nc.scalar.copy, w1_grouped[:, W1_BY_PAIRS:, :], w1_raw[:, :, W1_BY_PAIRS:])
+        for u in range(N // P):
+            cast_columns(nc.scalar.copy, w1_grouped[:, u * P : (u + 1) * P, :], w1_raw[:, u])
         relu_on_scalar(0)
         w1_codes, w1_plane = quantize(w1_grouped[:], "w1")
         relu_on_vector(1)

@@ -23,6 +23,7 @@ QUADRANT = 32
 QUADRANT_ROWS = 4
 TABLE_FIRST, TABLE_STEP = 32, 4
 GATHERS = ((0, 256), (256, 256), (512, 512))
+SHARED_TOKENS = 32
 GROUP = 128
 CHUNKS = ((0, 256), (256, 256), (512, 256), (768, 128), (896, 128))
 WARM_UP_PASSES = 4
@@ -129,14 +130,17 @@ def tile_picked_lora_relu_p_kernel(tc, x_words, x_scales, w1, w2, w3, offs, out)
             h_banks.append(bank_tile(bank, [SLOTS, GROUP]))
             hidden(group)
 
-        def h_views(group):
-            return h_grouped[:, group * GROUP : (group + 1) * GROUP, :], h_banks[group][:].rearrange("p t n -> p n t")
+        def h_views(group, lo, hi):
+            return (
+                h_grouped[:, group * GROUP + lo : group * GROUP + hi, :],
+                h_banks[group][:].rearrange("p t n -> p n t")[:, lo:hi, :],
+            )
 
-        def relu_on_scalar(group):
-            nc.scalar.activation(*h_views(group), RELU)
+        def relu_on_scalar(group, lo=0, hi=GROUP):
+            nc.scalar.activation(*h_views(group, lo, hi), RELU)
 
-        def relu_on_vector(group):
-            nc.vector.tensor_scalar_max(*h_views(group), 0.0)
+        def relu_on_vector(group, lo=0, hi=GROUP):
+            nc.vector.tensor_scalar_max(*h_views(group, lo, hi), 0.0)
 
         def quantize_h(chunk):
             first, count = CHUNKS[chunk]
@@ -206,7 +210,8 @@ def tile_picked_lora_relu_p_kernel(tc, x_words, x_scales, w1, w2, w3, offs, out)
         store_wide_chunk(0, out0)
         out2 = open_chunk(2, (7, 5))
         close_chunk(out2, quantize_h(2))
-        relu_on_vector(6)
+        relu_on_vector(6, 0, GROUP - SHARED_TOKENS)
+        relu_on_scalar(6, GROUP - SHARED_TOKENS, GROUP)
         store_wide_chunk(1, out1)
         out3 = open_chunk(3, (0, 1))
         relu_on_vector(7)

@@ -23,7 +23,7 @@ QUADRANT = 32
 QUADRANT_ROWS = 4
 TABLE_FIRST, TABLE_STEP = 32, 4
 GATHERS = ((0, 256), (256, 256), (512, 512))
-SHARED_TOKENS = 32
+SHARED_TOKENS = 16
 GROUP = 128
 CHUNKS = ((0, 256), (256, 256), (512, 256), (768, 128), (896, 128))
 WARM_UP_PASSES = 4

from contextlib import ExitStack

import concourse.mybir as mybir

K, T, S, H, N = 512, 4096, 1024, 512, 256
FLOPS = 2 * S * (K * H + K * N + H * N)

F32 = mybir.dt.float32
BF16 = mybir.dt.bfloat16
I32 = mybir.dt.int32
U32 = mybir.dt.uint32
U16 = mybir.dt.uint16
U8 = mybir.dt.uint8
FP8X4 = mybir.dt.float8_e4m3fn_x4
RELU = mybir.ActivationFunctionType.Relu

P = 128
DMA_BURST = 256
SLOTS = 4
BLOCKS = K // 32
LIST_ROWS = 16
QUADRANT = 32
QUADRANT_ROWS = 4
TABLE_FIRST, TABLE_STEP = 32, 4
GATHERS = ((0, 256), (256, 256), (512, 512))
SHARED_TOKENS = 16
GROUP = 128
CHUNKS = ((0, 256), (256, 256), (512, 256), (768, 128), (896, 128))
WARM_UP_PASSES = 4
WARM_UP_ROWS = 32


def tile_picked_lora_relu_p_kernel(tc, x_words, x_scales, w1, w2, w3, offs, out):
    nc = tc.nc
    with ExitStack() as ctx:
        keep = ctx.enter_context(tc.tile_pool(name="keep", bufs=1))
        psum = ctx.enter_context(tc.psum_pool(name="psum", bufs=1))

        def table_rows(first, count):
            return slice(TABLE_FIRST + first * TABLE_STEP, TABLE_FIRST + (first + count) * TABLE_STEP, TABLE_STEP)

        scale_table = keep.tile([P, T], U8, name="scale_table", align_bytes=DMA_BURST)
        nc.vector.memset(scale_table[:].bitcast(I32), 0)
        x_plane = keep.tile([P, S], U8, name="x_plane", align_bytes=DMA_BURST)
        nc.gpsimd.memset(x_plane[:].bitcast(I32), 0)

        word_table = keep.tile([P, T], I32, name="word_table", align_bytes=DMA_BURST)
        offsets = keep.tile([P, S // LIST_ROWS], U16, name="offsets", align_bytes=DMA_BURST)
        w2_raw = keep.tile([P, SLOTS, H], F32, name="w2_raw", align_bytes=DMA_BURST)
        nc.sync.dma_start(w2_raw[:], w2.rearrange("(p j) c -> p j c", j=SLOTS))
        nc.sync.dma_start(offsets[:], offs)
        nc.sync.dma_start(scale_table[table_rows(0, BLOCKS), :].bitcast(I32), x_scales[0].bitcast(I32))
        nc.sync.dma_start(word_table[:], x_words[0].rearrange("p n t -> p (n t)").bitcast(I32))

        picked_bytes = keep.tile([P, S], U8, name="picked_bytes", align_bytes=DMA_BURST)
        nc.vector.tensor_copy(picked_bytes[:], scale_table[:].indirect(offsets[:]))

        w1_rows = w1.rearrange("(p j) (u c) -> p u j c", j=SLOTS, c=P)
        w1_raw = keep.tile([P, N // P, SLOTS, P], F32, name="w1_then_h", align_bytes=DMA_BURST)
        nc.sync.dma_start(w1_raw[:, 0], w1_rows[:, 0])
        for q in range(P // QUADRANT):
            nc.sync.dma_start(
                x_plane[QUADRANT * q : QUADRANT * q + QUADRANT_ROWS, :].bitcast(I32),
                picked_bytes[table_rows(QUADRANT_ROWS * q, QUADRANT_ROWS), :].bitcast(I32),
            )
        nc.sync.dma_start(w1_raw[:, 1], w1_rows[:, 1])
        w3_raw = keep.tile([P, SLOTS, N], F32, name="w3_raw", align_bytes=DMA_BURST)
        nc.sync.dma_start(w3_raw[:], w3.rearrange("(p j) c -> p j c", j=SLOTS))

        def bank_tile(bank, shape):
            return psum.tile([P] + shape, F32, name=f"bank{bank}")

        def x_operand(first, count):
            g = max(i for i, (start, size) in enumerate(GATHERS) if start <= first)
            lo = first - GATHERS[g][0]
            return x_codes[g][:, lo : lo + count].bitcast(FP8X4), x_plane[:, first : first + count]

        w2_grouped = keep.tile([P, SLOTS, P, SLOTS], BF16, name="w2_grouped", align_bytes=64)

        def cast_columns(engine_copy, grouped, raw):
            engine_copy(
                grouped.rearrange("p (c i) j -> p c j i", i=2),
                raw.rearrange("p j (c i) -> p c j i", i=2),
            )

        w3_grouped = keep.tile([P, N, SLOTS], BF16, name="w3_grouped", align_bytes=64)
        w1_grouped = keep.tile([P, N, SLOTS], BF16, name="w1_grouped", align_bytes=64)

        def quantize(grouped, name):
            width = grouped.shape[1]
            codes = keep.tile([P, width], U32, name=name + "_codes", align_bytes=64)
            plane = keep.tile([P, width], U8, name=name + "_plane", align_bytes=64)
            nc.vector.quantize_mx(codes[:].bitcast(FP8X4), plane[:], grouped.rearrange("p c j -> p (c j)"))
            return codes, plane

        nc.scalar.copy(
            w2_grouped[:].rearrange("p t m j -> p m j t"),
            w2_raw[:].rearrange("p j (m t) -> p m j t", t=SLOTS),
        )
        w2_codes, w2_plane = quantize(w2_grouped[:].rearrange("p t m j -> p (t m) j"), "w2")

        warm_bank = bank_tile(7, [H])
        for warm_pass in range(WARM_UP_PASSES):
            nc.tensor.matmul_mx(
                warm_bank[:WARM_UP_ROWS, :], w2_codes[:, :WARM_UP_ROWS].bitcast(FP8X4), w2_plane[:, :WARM_UP_ROWS],
                w2_codes[:].bitcast(FP8X4), w2_plane[:], start=True, stop=True,
            )

        x_codes = []
        for g, (first, count) in enumerate(GATHERS):
            picked_words = keep.tile([P, count], U32, name=f"x_codes{g}", align_bytes=64)
            entries = slice(first // LIST_ROWS, (first + count) // LIST_ROWS)
            nc.vector.tensor_copy(picked_words[:], word_table[:].bitcast(U32).indirect(offsets[:, entries]))
            x_codes.append(picked_words)

        h_grouped = keep.tile([P, S, SLOTS], BF16, name="w1_then_h", align_bytes=DMA_BURST)
        early_groups = S // GROUP - 2
        h_banks = [bank_tile(group, [SLOTS, GROUP]) for group in range(early_groups)]

        def hidden(group):
            x_mx = x_operand(group * GROUP, GROUP)
            for t in range(SLOTS):
                cols = slice(t * P, (t + 1) * P)
                nc.tensor.matmul_mx(
                    h_banks[group][:, t, :], w2_codes[:, cols].bitcast(FP8X4), w2_plane[:, cols],
                    *x_mx, start=True, stop=True,
                )

        def late_hidden(group, bank):
            h_banks.append(bank_tile(bank, [SLOTS, GROUP]))
            hidden(group)

        def h_views(group, lo, hi):
            return (
                h_grouped[:, group * GROUP + lo : group * GROUP + hi, :],
                h_banks[group][:].rearrange("p t n -> p n t")[:, lo:hi, :],
            )

        def relu_on_scalar(group, lo=0, hi=GROUP):
            nc.scalar.activation(*h_views(group, lo, hi), RELU)

        def relu_on_vector(group, lo=0, hi=GROUP):
            nc.vector.tensor_scalar_max(*h_views(group, lo, hi), 0.0)

        def quantize_h(chunk):
            first, count = CHUNKS[chunk]
            return quantize(h_grouped[:, first : first + count, :], f"h{chunk}")

        out_rows = out.rearrange("(u p) s -> p u s", p=P)

        def open_chunk(chunk, banks):
            tiles = [bank_tile(bank, [CHUNKS[chunk][1]]) for bank in banks]
            for u, tile in enumerate(tiles):
                cols = slice(u * P, (u + 1) * P)
                nc.tensor.matmul_mx(
                    tile[:], w1_codes[:, cols].bitcast(FP8X4), w1_plane[:, cols],
                    *x_operand(*CHUNKS[chunk]), start=True, stop=False,
                )
            return tiles

        def close_chunk(tiles, h_mx):
            h_codes, h_plane = h_mx
            for u, tile in enumerate(tiles):
                w3_codes, w3_plane = w3_mx[u]
                nc.tensor.matmul_mx(
                    tile[:], w3_codes[:].bitcast(FP8X4), w3_plane[:],
                    h_codes[:].bitcast(FP8X4), h_plane[:], start=False, stop=True,
                )

        staged = keep.tile([P, N // P, S], F32, name="staged", align_bytes=DMA_BURST)

        def empty(engine_copy, chunk, tiles, u):
            first, count = CHUNKS[chunk]
            engine_copy(staged[:, u, first : first + count], tiles[u][:])

        def store_wide_chunk(chunk, tiles):
            first, count = CHUNKS[chunk]
            for u in range(N // P):
                empty(nc.scalar.copy, chunk, tiles, u)
                nc.sync.dma_start(out_rows[:, u, first : first + count], staged[:, u, first : first + count])

        def store_short_chunk(chunk, tiles):
            first, count = CHUNKS[chunk]
            empty(nc.vector.tensor_copy, chunk, tiles, 0)
            empty(nc.scalar.copy, chunk, tiles, 1)
            nc.sync.dma_start(out_rows[:, :, first : first + count], staged[:, :, first : first + count])

        for group in range(early_groups):
            hidden(group)

        for u in range(N // P):
            cast_columns(nc.scalar.copy, w1_grouped[:, u * P : (u + 1) * P, :], w1_raw[:, u])
        relu_on_scalar(0)
        w1_codes, w1_plane = quantize(w1_grouped[:], "w1")
        relu_on_vector(1)
        relu_on_scalar(2)
        cast_columns(nc.vector.tensor_copy, w3_grouped[:], w3_raw[:])
        relu_on_scalar(3)
        h_mx0 = quantize_h(0)
        relu_on_scalar(4)
        w3_mx = [quantize(w3_grouped[:, u * P : (u + 1) * P, :], f"w3_{u}") for u in range(N // P)]

        out0 = open_chunk(0, (0, 1))
        late_hidden(6, 3)
        close_chunk(out0, h_mx0)
        out1 = open_chunk(1, (2, 6))
        late_hidden(7, 4)
        relu_on_scalar(5)
        close_chunk(out1, quantize_h(1))
        store_wide_chunk(0, out0)
        out2 = open_chunk(2, (7, 5))
        close_chunk(out2, quantize_h(2))
        relu_on_vector(6, 0, GROUP - SHARED_TOKENS)
        relu_on_scalar(6, GROUP - SHARED_TOKENS, GROUP)
        store_wide_chunk(1, out1)
        out3 = open_chunk(3, (0, 1))
        relu_on_vector(7)
        close_chunk(out3, quantize_h(3))
        out4 = open_chunk(4, (2, 6))
        store_wide_chunk(2, out2)
        close_chunk(out4, quantize_h(4))
        store_short_chunk(3, out3)
        store_short_chunk(4, out4)
